import numpy as np, ml_dtypes
CORES = [24,25,26,27,28,29,30,31]
N = 8
import mx_ref
BF = ml_dtypes.bfloat16
def gentries(a):
    return np.ascontiguousarray(a.reshape(8, 16, -1).transpose(0, 2, 1)).reshape(8, -1)
def gtable(e):
    e = np.asarray(e); return np.ascontiguousarray(e.reshape(8, -1, 16).transpose(0, 2, 1)).reshape(128, -1).astype(np.int32)
def gcols(t, e):
    v = np.concatenate([t.reshape(8, 16, -1, 4), np.zeros((8, 16, 1, 4), BF)], axis=2)
    return np.ascontiguousarray(np.stack([v[g][:, e[g]] for g in range(8)])).reshape(128, -1)
def tile(rs):
    return np.stack(rs, axis=2).reshape(128, -1).astype(BF)
def pick(q, e):
    c = np.concatenate([q[0].reshape(128, -1, 4), np.zeros((128, 1, 4), np.uint8)], axis=1); s = np.concatenate([q[1], np.ones((16, 1), np.uint8)], axis=1)
    return (np.ascontiguousarray(c[:, e].reshape(128, -1)), np.ascontiguousarray(s[:, e]))
def join(*qs):
    return (np.concatenate([q[0] for q in qs], axis=1), np.concatenate([q[1] for q in qs], axis=1))
def put(q, e, v):
    c, s = q[0].reshape(128, -1, 4).copy(), q[1].copy(); c[:, e] = v[0].reshape(128, -1, 4); s[:, e] = v[1]
    return (c.reshape(128, -1), s)
def pk(c, s):
    return (np.ascontiguousarray(c), mx_ref.live(s))
def emit(q):
    return q[0], q[1]
def packed(v, rng):
    q = [mx_ref.quantize(np.ascontiguousarray(v[r])) for r in range(N)]
    return np.stack([a for a, b in q]), np.stack([mx_ref.plane(b, rng) for a, b in q])
def values_of_codes():
    e, c = np.zeros((128, 128, 4), np.float32), np.zeros((128, 2, 4), np.uint8)
    e[np.arange(128), np.arange(128), 0] = 1
    c[:127, :, 0] = np.arange(256).reshape(2, 128).T[:127]
    return mx_ref.matmul(mx_ref.quantize(e.reshape(128, 512).astype(BF)), (c.reshape(128, 8), np.full((16, 2), 127, np.uint8))).T.reshape(-1).astype(np.float64)
CODE_VALUE, SCALE_VALUE = values_of_codes(), 2.0 ** (np.arange(256) - 127.0)
def decode(q):
    return (CODE_VALUE[q[0]].reshape(16, 8, -1, 4) * SCALE_VALUE[q[1]][:, None, :, None] + 0.0).reshape(128, -1).astype(np.float32)
def f(rng, *shape):
    return mx_ref.flush((rng.standard_normal(shape, dtype=np.float32) * np.exp2(rng.integers(-2, 3, shape[:-1] + (1,)))).astype(BF))
def wide(rng, *shape, cols=0):
    v = rng.standard_normal(shape, dtype=np.float32) * np.exp2(rng.integers(-12, 13, shape)).astype(np.float32)
    if cols: v *= np.repeat(np.exp2(rng.integers(-cols, cols + 1, shape[:-2] + (1, shape[-1] // 4))) * (rng.random(shape[:-2] + (1, shape[-1] // 4)) > 0.0625), 4, axis=-1).astype(np.float32)
    return mx_ref.flush(v.astype(BF))
C, M, R = 256, 128, 3
SH = (N, 8, 2, C, 4)
def numbers_of(rng):
    return {"x": np.array(f(rng, N, 128, 4 * C)), "u": np.array(f(rng, N, 128, 512)), "v": np.array(f(rng, N, 128, 512))}
def lists_of(e, c, a):
    return {"al": np.stack([gtable(e[r]) for r in range(N)]), "nx": np.stack([gtable((512 * c + a)[r].reshape(8, 8 * C)) for r in range(N)])}
def lists(rng):
    return lists_of(rng.integers(0, C, (N, 8, C)), rng.integers(0, 5, SH), rng.integers(0, C, SH))
def layers(rng, still=0):
    w = np.array(f(rng, N, 128, 2048)).reshape(N, 8, 16, 4, 8, 16, 4)
    w[:, :, :still] = 0
    w[:, :, :, :, :, :still] = 0
    return w
def weights(rng, w):
    c, s = packed(np.ascontiguousarray(w).reshape(N, 128, 2048), rng)
    return {"wc": c, "ws": s}
def setup_inputs(rng):
    return {**numbers_of(rng), **lists(rng), **weights(rng, layers(rng))}
def setup_inputs_near(rng):
    d = numbers_of(rng)
    x = d["x"].reshape(N, 8, 16, C, 4)
    u = d["u"].reshape(N, 128, 128, 4)
    o = rng.permutation(N) % 2
    x[:, :, :8] = 0
    u[:, :, ::16] = 0
    u[:, :, 1::16] = 0
    for r in range(N):
        k = 2.0 ** -30 if o[r] == 0 else 1.0
        s = rng.integers(-1, 2, (8, 2, C)) * k
        for g in rng.permutation(8)[:4]: s[g, :, rng.integers(C)] = 2.0 ** 14 * rng.choice([-1.0, 1.0], 2)
        x[r, :, :2, :, 0] = s.astype(np.float32).astype(BF)
        t = np.where(s[:, 0] == 0, rng.integers(-1, 2, (8, C)), 0) * k
        x[r, :, 2, :, 0] = (1.125 * t).astype(np.float32).astype(BF)
        x[r, :, 3, :, 0] = (-t).astype(np.float32).astype(BF)
        for h in [0, 16, 32, 48, 64, 80, 96, 112, 1, 17]:
            u[r, h, h, 0] = k
            u[r, h - h % 16 + 2, h, 0] = 1.125 * k
            u[r, h - h % 16 + 3, h, 0] = 1.25 * k
    return {"x": x.reshape(N, 128, 4 * C), "u": u.reshape(N, 128, 512), "v": d["v"], **lists(rng), **weights(rng, layers(rng, 8))}
def setup_inputs_chain(rng):
    d = numbers_of(rng)
    e = rng.permutation(N)
    c = rng.integers(0, 5, SH)
    i = np.arange(4)
    c[e[0]] = rng.integers(1, 5, SH[1:])
    c[e[1]] = 0
    c[e[2]] = np.where(np.arange(8)[:, None] <= 2 * i, i + 1, 0)[:, None, None, :]
    c[e[3]][:, 0] = 0
    c[e[3]][:, 1] = rng.integers(1, 5, (8, C, 4))
    return {**d, **lists_of(rng.integers(0, C, (N, 8, C)), c, rng.integers(0, C, SH)), **weights(rng, layers(rng))}
def setup_inputs_twice(rng):
    d = numbers_of(rng)
    s = 2.0 ** -rng.integers(8, 15, (N, 16, C, 32)) * (1.125 + 0.25 * rng.integers(0, 4, (N, 16, C, 32)))
    s[:, :, :, 4] = 2.0 ** -rng.integers(8, 12, (N, 16, C)) * (1.125 + 0.25 * rng.integers(0, 4, (N, 16, C)))
    np.put_along_axis(s, rng.integers(8, 32, (N, 16, C, 1)), 1.96875, axis=3)
    s = s * rng.choice([-1.0, 1.0], s.shape)
    s[:, :, :, 0] = 0.125 * s[:, :, :, 4]
    s = s * np.exp2(rng.integers(10, 13, (N, 16, C, 1)))
    x = np.ascontiguousarray(s.reshape(N, 16, C, 8, 4).transpose(0, 1, 3, 2, 4)).reshape(N, 128, 4 * C)
    u = d["u"].reshape(N, 128, 128, 4)
    u[:, :, ::16] = 0
    for h in range(0, 128, 16):
        u[:, h, h, 0] = 1.0
        u[:, h + 1, h, 0] = -0.125
    w = np.array(mx_ref.flush((layers(rng).astype(np.float32) * np.float32(2.0 ** -12)).astype(BF))).reshape(N, 128, 4, 128, 4)
    i = np.arange(128)
    for b in range(4): w[:, i, b, i, b] = -1.0
    return {"x": x.astype(np.float32).astype(BF), "u": u.reshape(N, 128, 512), "v": d["v"], **lists(rng), **weights(rng, w)}
def setup_inputs_ends(rng):
    d = numbers_of(rng)
    e = rng.permutation(N)
    x = d["x"].reshape(N, 8, 16, C, 4)
    u = d["u"].reshape(N, 128, 128, 4)
    v = d["v"].reshape(N, 128, 128, 4)
    t = np.clip(rng.integers(-C, 2 * C, (N, 8, C)), 0, C - 1)
    c = 4 * rng.integers(0, 2, SH)
    a = np.clip(rng.integers(-C, 2 * C, SH), 0, C - 1)
    t[e[0]], c[e[0]], a[e[0]] = C - 1, 4, C - 1
    t[e[1]], c[e[1]], a[e[1]] = 0, 0, 0
    u[:, :, ::16] = 0
    u[:, :, 1::16] = 0
    for i in range(N):
        r = e[i]
        s = rng.integers(-1, 2, (8, C)) * 1.0
        s[rng.permutation(8)[:2]] = rng.choice([-1.0, 1.0], (2, 1))
        s = s * (2.0 ** -30 if i % 2 else 2.0 ** 14)
        x[r, :, :8] = s[:, None, :, None].astype(np.float32).astype(BF)
        for h in [0, 16, 32, 48, 64, 80, 96, 112, 1, 17]: u[r, h - h % 16:h - h % 16 + 8, h] = 2.0 ** -30 if i % 2 else 2.0 ** 30
    x[e[0]] = (2.0 ** 14 * rng.choice([-1.0, 1.0], (C, 1))).astype(np.float32).astype(BF)
    u[e[0]] = (2.0 ** 30 * rng.choice([-1.0, 1.0], (128, 1))).astype(np.float32).astype(BF)
    v[e[0]] = (2.0 ** 30 * rng.choice([-1.0, 1.0], (128, 1))).astype(np.float32).astype(BF)
    w = layers(rng, 8)
    w[e[0]][:, 8:, :, :, 8:] = 8
    w[e[1]] = 0
    v = (np.where(v < 0, -1.0, 1.0) * np.where(rng.permutation(N) % 2, 2.0 ** -30, 2.0 ** 30)[:, None, None, None]).astype(np.float32).astype(BF)
    return {"x": x.reshape(N, 128, 4 * C), "u": u.reshape(N, 128, 512), "v": v.reshape(N, 128, 512), **lists_of(t, c, a), **weights(rng, w)}
def setup_inputs_spread(rng):
    d = setup_inputs(rng)
    d["x"] = mx_ref.flush((wide(rng, N, 128, 4 * C, cols=6).astype(np.float32) * np.float32(2.0 ** -7)).astype(BF))
    return d
def check_inputs(d):
    b = []
    for k, most in (("x", 2.0 ** 14), ("u", 2.0 ** 30), ("v", 2.0 ** 30)):
        a = np.abs(d[k].astype(np.float32))
        if not (np.isfinite(a).all() and ((a == 0) | (a >= 2.0 ** -30) & (a <= most)).all()): b.append("a value of " + k)
    if not ((d["al"] >= 0) & (d["al"] < C)).all(): b.append("an entry of al")
    if not ((d["nx"] >= 0) & (d["nx"] < 2560) & (d["nx"] % 512 < C)).all(): b.append("an entry of nx")
    none, least, most = [emit(mx_ref.quantize(np.full((128, 16), k, np.float32).astype(BF)))[1][0, 0] for k in (0.0, 2.0 ** -30, 2.0 ** 30)]
    for r in range(N):
        if ((d["wc"][r] == 0x7F) | (d["wc"][r] == 0xFF)).any(): b.append("wc: a code that is no number")
        s = mx_ref.live(d["ws"][r])
        if ((s != none) & ((s < least) | (s > most))).any(): b.append("ws: a scale out of range")
        w = np.abs(decode(pk(d["wc"][r], d["ws"][r])).astype(np.float64)).reshape(128, 512, 4)
        if not (np.sum(w, axis=(0, 2)) <= 2048).all(): b.append("a column of W adds up to more than 2048")
    return b
def reference(x, u, v, al, nx, wc, ws):
    qu = [mx_ref.quantize(u[r]) for r in range(N)]
    lay = [pk(wc[r], ws[r]) for r in range(N)]
    now = [x[r] for r in range(N)]
    ad = np.stack([gentries(al[r]) for r in range(N)])
    follow = [gentries(nx[r]) for r in range(N)]
    for t in range(R):
        made = []
        for r in range(N):
            q = mx_ref.quantize(now[r])
            s = mx_ref.matmul(qu[r], q)
            edge = 2 * (s[1] > 0) + (s[17] > 0)
            on = np.ones(C, bool)
            for g in range(8):
                bit = s[16 * g][ad[r, g]] > 0
                n = follow[r][g][4 * C * bit + 4 * ad[r, g] + edge]
                ad[r, g] = np.where(on, n % 512, ad[r, g])
                on = on & (n >= 512)
                edge = np.where(on, n // 512 - 1, 0)
            made.append(mx_ref.quantize(gcols(decode(q).astype(BF), ad[r])))
        ad[:, :, C - M:] = np.roll(ad[:, :, C - M:], 1, axis=0)
        for r in range(N):
            q = join(pick(made[r], np.arange(C - M)), pick(made[r - 1], np.arange(C - M, C)))
            own = decode(q)
            now[r] = tile([mx_ref.matmul(pick(lay[r], np.arange(128 * b, 128 * b + 128)), q) * np.float32(0.015625) + own[:, b::4] for b in range(4)])
    y, oa = np.zeros((N, 128, C), np.float32), np.zeros((N, 8, C), np.float32)
    oc, osc = np.zeros((N, 128, 4 * C), np.uint8), np.zeros((N, 16, C), np.uint8)
    for r in range(N):
        q = mx_ref.quantize(now[r])
        y[r] = mx_ref.matmul(mx_ref.quantize(v[r]), q)
        oa[r] = ad[r]
        oc[r], osc[r] = emit(q)
    return {"y": y, "oa": oa, "oc": oc, "osc": osc}

@@ -1,0 +1,360 @@
+from concourse.mybir import dt, AluOpType, AxisListType, ActivationFunctionType
+
+A = AluOpType
+COPY = ActivationFunctionType.Copy
+R = 3
+SCRATCH = {}
+for _d, _l in (
+        ("int32", "nx4:512 ep:512 e8:128 ep2:256 pp:128 ai0:128 ai:128 n4i:512 sl:256 slt:256 ip:8 iph:8 iy:2 k0:64 pc:32 ei:128 am:16"),
+        ("float32", "p4:128 pr:256 pw:256 nw:2304 kf:64 mi:16 tb:16 oh:16 sc:1 cst:32 geo:32 ss:128 key:128 norm:16 nb:16 pg:256 pt:256 "
+                    "ek:128 dd:128 yi:16 tmp:128 wk:112 oaf:256 ys:256"),
+        ("bfloat16", "n4:512 nr:2048 i64:128 c64:128 et:2048 ut:512 vt:512 sb:256 bg:288 bt:288 nbf:256 at:256 val:16 f0:1024 f1:1024 "
+                     "f2:1024 co0:16 co1:16 ca0:16 ca1:16 xl0:512 xl1:512 xl2:512 xl3:512 xh0:512 xh1:512 xh2:512 xh3:512 "
+                     "zl0:512 zl1:512 zl2:512 zh0:512 zh1:512 zh2:512"),
+        ("uint16", "ul:8 lb:18 ou:16 nu:256 ga:8 gl0:16 gl1:16 gl2:16")):
+    for _s in _l.split():
+        SCRATCH[_s.split(":")[0]] = ("sbuf", [128, int(_s.split(":")[1])], _d)
+for _s in "qe:512 lw:512 qu:128 qy:128 qv:128 qx:256:4 qh:128:3 ql:128:3 qa:128:3".split():
+    _p = _s.split(":")
+    for _t in ([""] if len(_p) == 2 else ["%d" % k for k in range(int(_p[2]))]):
+        SCRATCH[_p[0] + _t] = ("sbuf", [128, int(_p[1])], "float8_e4m3fn_x4")
+        SCRATCH[_p[0] + "s" + _t] = ("sbuf", [128, int(_p[1])], "uint8")
+BANK = ["b%d" % k for k in range(10, 18)]
+for _s in BANK:
+    SCRATCH[_s] = ("psum", [128, 512], "float32")
+SEMAPHORES = ("cv cs ct cg dnx dal dx du dv dw dpr dnr dyl dyh doa docl doch dgl0 dgl1 dgl2".split()
+              + [n + "%d" % t for n in ("rl", "ll", "rc", "lc", "rs", "ls") for t in range(R)])
+
+
+def rank_program(g, core, T, topo):
+    rank = T.rank_of(core)
+    if rank is None:
+        return
+    nxt = T.cores[(rank + 1) % len(T.cores)]
+    rid, pid, _ = topo.addr(nxt)
+    mask, neng = topo.mask(core, nxt), len(topo.engines(core, nxt))
+    V, S, P = g.vector, g.scalar, g.tensor
+    eng = {"v": V, "s": S, "t": P, "g": g, "y": g.sync}
+    csem = {"v": "cv", "s": "cs", "t": "ct", "g": "cg"}
+    cnt, wr, rd = {}, {}, {}
+    known = {q: {} for q in eng}
+
+    def deps(q, r, w):
+        toks = [wr[k] for k in r if k in wr]
+        for k in w:
+            toks += rd.get(k, []) + ([wr[k]] if k in wr else [])
+        toks = [t for t in toks if known[q].get(t[0], 0) < t[1]]
+        best = {}
+        for t in toks:
+            if t[0] not in best or best[t[0]][1] < t[1]:
+                best[t[0]] = t
+        for t in list(best.values()):
+            if not any(o is not t and o[2].get(t[0], 0) >= t[1] for o in best.values()):
+                eng[q].wait_ge(T.sem[t[0]], t[1])
+        for t in toks:
+            for s, n in list(t[2].items()) + [(t[0], t[1])]:
+                known[q][s] = max(known[q].get(s, 0), n)
+
+    def note(tok, r, w):
+        for k in r:
+            rd.setdefault(k, []).append(tok)
+        for k in w:
+            wr[k] = tok
+            rd[k] = []
+
+    def op(q, fn, r, w):
+        r, w = r.split(), w.split()
+        w = w + [k for k in r if k in BANK]
+        deps(q, r, w)
+        s = csem[q]
+        cnt[s] = cnt.get(s, 0) + 1
+        fn().then_inc(T.sem[s], 1)
+        clk = dict(known[q])
+        clk[s] = cnt[s]
+        note((s, cnt[s], clk), r, w)
+
+    def dmas(sem, lst, r, w):
+        r, w = r.split(), w.split()
+        qs = sorted(set(q for q, _, _ in lst))
+        for q in qs:
+            deps(q, r, w)
+        for q, o, i in lst:
+            cnt[sem] = cnt.get(sem, 0) + 16
+            eng[q].dma_start(o, i).then_inc(T.sem[sem], 16)
+        clk = {sem: cnt[sem]}
+        for q in qs:
+            for s, n in known[q].items():
+                clk[s] = max(clk.get(s, 0), n)
+        note((sem, cnt[sem], clk), r, w)
+
+    def send(out, inp, rs, ls, r, lands):
+        deps("g", [r], [])
+        g.remote_dma(out, inp, T.sem[rs], T.sem[ls], pid, rid, mask)
+        for s in (ls, rs):
+            cnt[s] = cnt.get(s, 0) + neng
+        note((ls, cnt[ls], {}), [r], [])
+        note((rs, cnt[rs], {}), [], [lands])
+
+    def vs(out, i, s1, s2, o1, r, w, o2=None):
+        if o2 is None:
+            op("v", lambda: V.tensor_scalar(out, i, s1, None, o1), r, w)
+        else:
+            op("v", lambda: V.tensor_scalar(out, i, s1, s2, o1, o2), r, w)
+
+    def vt(out, a, b, o, r, w):
+        op("v", lambda: V.tensor_tensor(out, a, b, o), r, w)
+
+    def vc(out, i, r, w):
+        op("v", lambda: V.tensor_copy(out, i), r, w)
+
+    def ac(out, i, r, w, scale=None):
+        if scale is None:
+            op("s", lambda: S.activation(out, i, COPY), r, w)
+        else:
+            op("s", lambda: S.activation(out, i, COPY, scale=scale), r, w)
+
+    def fill(ap, c, w):
+        op("v", lambda: V.memset(ap, c), "", w)
+
+    def quant(o, s, i, r, w):
+        op("v", lambda: V.quantize_mx(o, s, i), r, w)
+
+    def turn(o, i, r, w):
+        op("v", lambda: V.transpose(o, i), r, w)
+
+    def iota(o, pat, cm, w, small=False):
+        if small:
+            op("g", lambda: g.iota(o, pat, 0, cm, allow_small_or_imprecise_dtypes=True), "", w)
+        else:
+            op("g", lambda: g.iota(o, pat, 0, cm), "", w)
+
+    def mm(bank, n, l, ls, rh, rs, r, start=True, stop=True):
+        op("t", lambda: P.matmul_mx(T[bank][:, 0:n], l, ls, rh, rs, start, stop), r, bank)
+
+    k0, kf, wk = T.k0, T.kf, T.wk
+    dmas("dnx", [("ys"[e // 2], T.nx4[0:32, 128 * e:128 * e + 128], T.nx[e:128:4, :]) for e in range(4)], "", "nx4")
+    dmas("dx", [("y", T.xl0[:], T.x[:, 0:512]), ("s", T.xh0[:], T.x[:, 512:1024])], "", "xl0 xh0")
+    dmas("du", [("y", T.ut[:], T.u[:])], "", "ut")
+    fill(T.sl[:], 0, "sl")
+    fill(T.c64[:], 64.0, "c64")
+    dmas("dal", [("sy"[k % 2], T.sl[2 * k:128:16, 32 * k:32 * k + 32], T.al[16 * k:16 * k + 16, :]) for k in range(8)], "", "sl")
+    dmas("dw", [("y", T.lw[:].bitcast(dt.uint8), T.wc[:]), ("s", T.lws[:], T.ws[:])], "", "lw")
+    dmas("dv", [("y", T.vt[:], T.v[:])], "", "vt")
+
+    iota(T.ip[:], [[0, 8]], 1, "ip")
+    iota(T.ai0[0:32, :], [[0, 2], [4, 64]], 0, "ai0")
+    iota(T.iph[:], [[1, 8]], 1, "iph")
+    iota(T.iy[:], [[2, 2]], 16, "iy")
+    iota(T.mi[:], [[1, 16]], 0, "mi", True)
+    op("g", lambda: g.affine_select(T.i64[:], T.c64[:], [[-1, 128]], A.is_equal, 0.0, 0, 1), "c64", "i64")
+    iota(T.key[:], [[16, 4], [256, 2], [0, 16]], 0, "key", True)
+    iota(T.et[:], [[0, 2048]], 0, "et", True)
+    iota(T.nw[:, 2048:2304], [[1, 256]], 0, "nwi", True)
+
+    fill(T.cst[:, 0:8], 0.0625, "cst0")
+    fill(T.cst[:, 8:16], 16.0, "cst1")
+    fill(T.cst[:, 16:24], 0.0, "cst2")
+    fill(T.tb[:], 0.0, "tb")
+    vs(k0[:, 0:1], T.ip[:, 0:1], 3, None, A.bitwise_and, "ip", "k0a")
+    vc(kf[:, 0:1], k0[:, 0:1], "k0a", "kfa")
+    vs(T.ai[0:32, :], T.ai0[0:32, :], kf[0:32, 0:1], 65536.0, A.add, "ai0 kfa", "aix", A.mult)
+    vs(T.ai[0:32, :], T.ai[0:32, :], 7 * 4369.0, None, A.add, "aix", "ai")
+    vs(k0[:, 8:16], T.ip[:], 14, None, A.bitwise_and, "ip", "k0b")
+    vs(k0[:, 16:17], T.ip[:, 0:1], 4, 1, A.logical_shift_right, "ip", "k0d", A.bitwise_and)
+    vs(k0[:, 24:32], T.iph[:], 1, None, A.bitwise_and, "iph", "k0c")
+    vs(kf[:, 8:16], k0[:, 8:16], 8.0, None, A.mult, "k0b", "kfb")
+    vt(kf[:, 16:24], kf[:, 8:16], k0[:, 24:32], A.add, "kfb k0c", "kfc")
+    vc(T.ul[:], kf[:, 16:24], "kfc", "ul")
+    op("v", lambda: V.tensor_tensor_scan(T.geo[:, 0:8], T.cst[:, 0:8], T.cst[:, 16:24], 4096.0, A.mult, A.add), "cst0 cst2", "geo0")
+
+    for e in range(4):
+        a = slice(128 * e, 128 * e + 128)
+        if e < 3:
+            vs(T.ep[0:32, a], T.nx4[0:32, a], 9 - 4 * e, 7 << (4 * e), A.logical_shift_right, "nx4", "ep%d" % e, A.bitwise_and)
+        else:
+            vs(T.e8[0:32, :], T.nx4[0:32, a], 8.0, None, A.mult, "nx4", "e8")
+            vs(T.ep[0:32, a], T.e8[0:32, :], 7 << 12, None, A.bitwise_and, "e8", "ep3")
+    vt(T.ep2[0:32, :], T.ep[0:32, 0:256], T.ep[0:32, 256:512], A.add, "ep0 ep1 ep2 ep3", "epx")
+    vt(T.pp[0:32, :], T.ep2[0:32, 0:128], T.ep2[0:32, 128:256], A.add, "epx", "pp")
+    vt(T.p4[0:32, :], T.pp[0:32, :], T.ai[0:32, :], A.add, "pp ai", "p4")
+    lst = []
+    for H in range(8):
+        for b in range(2):
+            z = (b + H) % 2
+            lst.append(("sy"[b], T.pr[16 * H + z:16 * H + 16:2, :], T.p4[0:32, 64 * b:64 * b + 64]))
+    dmas("dpr", lst, "p4", "pr")
+    vs(T.n4i[0:32, :], T.nx4[0:32, :], 511, None, A.bitwise_and, "nx4", "n4i")
+    vc(T.n4[0:32, :], T.n4i[0:32, :], "n4i", "n4")
+    dmas("dnr", [("sy"[z], T.nr[16 * H + z:16 * H + 16:2, :], T.n4[0:32, :]) for H in range(8) for z in range(2)], "n4", "nr")
+
+    turn(T.slt[:], T.sl[:], "sl", "slt")
+    vc(T.lb[:, 0:16:2], T.slt[:, 0:256:34], "slt", "lb0")
+    vc(T.lb[:, 1:16:2], T.slt[:, 16:256:34], "slt", "lb1")
+    quant(T.qu[:], T.qus[:], T.ut[:], "ut", "qu")
+    vc(T.qy[:].bitcast(dt.uint32), T.qu[:].bitcast(dt.uint32).indirect(T.ul[:]), "qu ul", "qy")
+    ac(T.qys[:], T.qus[:].indirect(T.ul[:]), "qu ul", "qys")
+    quant(T.qx0[:, 0:128], T.qxs0[:, 0:128], T.xl0[:], "xl0", "qx0L")
+    quant(T.qx0[:, 128:256], T.qxs0[:, 128:256], T.xh0[:], "xh0", "qx0H")
+    for r in range(4):
+        vc(T.pw[:, r:256:4], T.pr[:, 64 * r:64 * r + 64], "pr", "pw%d" % r)
+
+    def prefetch_pick():
+        ac(T.pg[:], T.pw[:].indirect(T.lb[:, 0:16]), "pw0 pw1 pw2 pw3 lb0 lb1", "pg")
+
+    prefetch_pick()
+    fill(T.tb[:, 1:2], 32.0, "tb")
+    fill(T.tb[:, 3:4], 16.0, "tb")
+    vc(T.tb[:, 0:16:2], T.geo[:, 0:8], "geo0", "tb")
+    vt(kf[:, 49:50], k0[:, 24:25], k0[:, 16:17], A.not_equal, "k0c k0d", "kfh")
+    vt(kf[:, 50:51], k0[:, 8:9], kf[:, 49:50], A.add, "k0b kfh", "kfi")
+    vs(T.oh[:], T.mi[:], kf[:, 50:51], None, A.is_equal, "mi kfi", "oh")
+    vt(T.oh[:], T.oh[:], T.tb[:], A.mult, "oh tb", "oh")
+    op("v", lambda: V.tensor_reduce(T.sc[:], T.oh[:], AxisListType.X, A.add), "oh", "sc")
+    for y in range(2):
+        vs(T.ss[:, y:16:2], T.geo[:, 0:8], 2.0 ** -8, None, A.mult, "geo0", "ss%d" % y)
+    vc(T.ss[:, 16:32], T.ss[:, 0:16], "ss0 ss1", "ss2")
+    vc(T.ss[:, 32:64], T.ss[:, 0:32], "ss0 ss1 ss2", "ss3")
+    vc(T.ss[:, 64:128], T.ss[:, 0:64], "ss0 ss1 ss2 ss3", "ss4")
+    for b in range(4):
+        ac(T.et[:, 512 * b + b:512 * b + 512:4], T.i64[:], "i64 et", "et_%d" % b)
+
+    def prefetch_rest():
+        turn(T.pt[:], T.pg[:], "pg", "pt")
+        vc(T.pc[:, 0:16], T.pt[:, 0:256:17], "pt", "pc0")
+        vc(T.pc[:, 16:32:2], T.pt[:, 1:256:34], "pt", "pc1")
+        vc(T.pc[:, 17:32:2], T.pt[:, 16:256:34], "pt", "pc2")
+        for e in range(4):
+            vs(T.ei[:, 32 * e:32 * e + 32], T.pc[:], 4 * e, 7, A.logical_shift_right, "pc0 pc1 pc2", "ei%d" % e, A.bitwise_and)
+        vt(T.ek[:], T.ei[:], T.key[:], A.add, "ei0 ei1 ei2 ei3 key", "ek")
+        vt(T.dd[:], T.ek[:], T.ss[:], A.mult, "ek ss0 ss1 ss2 ss3 ss4", "dd")
+        vs(T.am[:], T.pc[:, 0:16], 16, None, A.logical_shift_right, "pc0", "am")
+        vs(T.yi[:], T.am[:], 2048.0, None, A.add, "am", "yi")
+
+    def table_part(r):
+        (ac if r else vc)(T.nw[:, r:2048:4], T.nr[:, 512 * r:512 * r + 512], "nr", "nw%d" % r)
+
+    def score_mm(t, h):
+        a = slice(128 * h, 128 * h + 128)
+        mm(BANK[h], 128, T.qy[:], T.qys[:], T["qx%d" % t][:, a], T["qxs%d" % t][:, a], "qy qys qx%d" % t + "LH"[h])
+
+    def score_bits(h):
+        vs(T.sb[:, 128 * h:128 * h + 128], T[BANK[h]][:, 0:128], 0.0, T.sc[:], A.is_gt, BANK[h] + " sc", "sb%d" % h, A.mult)
+
+    def unpack(t):
+        for b in range(4):
+            a = slice(128 * b, 128 * b + 128)
+            mm(BANK[2 + b], 256, T.qe[:, a], T.qes[:, a], T["qx%d" % t][:], T["qxs%d" % t][:], "qe qx%dL qx%dH" % (t, t))
+        for b in range(4):
+            ac(T["f%d" % t][:, 256 * b:256 * b + 256], T[BANK[2 + b]][:, 0:256], BANK[2 + b], "f%d_%d" % (t, b), 0.015625)
+
+    score_mm(0, 0)
+    score_mm(0, 1)
+    vs(k0[:, 32:34], T.ip[:, 0:2], 4, None, A.logical_shift_right, "ip", "k0e")
+    vs(kf[:, 32:34], k0[:, 32:34], -254.0, None, A.mult, "k0e", "kfe")
+    vt(kf[:, 34:36], kf[:, 32:34], T.iy[:], A.add, "kfe iy", "kff")
+    vc(kf[:, 40:41], k0[:, 16:17], "k0d", "kfd")
+    vs(T.lb[:, 16:18], kf[:, 34:36], kf[:, 40:41], None, A.subtract, "kff kfd", "lbj")
+    score_bits(0)
+    score_bits(1)
+    prefetch_rest()
+
+    for t in range(R):
+        ts = "%d" % t
+        gl, f = T["gl" + ts], T["f" + ts]
+        vc(T.bg[:], T.sb[:].indirect(T.lb[:]), "sb0 sb1 lb0 lb1 lbj", "bg")
+        if t == 0:
+            for r in (1, 2, 3):
+                table_part(r)
+            quant(T.qe[:], T.qes[:], T.et[:], "et et_0 et_1 et_2 et_3", "qe")
+            op("v", lambda: V.tensor_tensor_scan(T.geo[:, 8:16], T.cst[:, 8:16], T.cst[:, 16:24], 2.0, A.mult, A.add), "cst1 cst2", "geo1")
+            for y in range(2):
+                vc(T.norm[:, y:16:2], T.geo[:, 8:16], "geo1", "norm%d" % y)
+            vs(T.nb[:], T.norm[:], 2.0 ** -5, None, A.mult, "norm0 norm1", "nb")
+        unpack(t)
+        turn(T.bt[:], T.bg[:], "bg", "bt")
+        vt(T.val[:, 0:2], T.bt[:, 257:273:15], T.bt[:, 259:275:15], A.add, "bt", "val0 val1")
+        for i in range(14):
+            vs(T.tmp[:, 8 * i:8 * i + 8], T.dd[:, i:128:16], T.val[:, i:i + 1], T.bt[:, 17 * i:17 * i + 1], A.subtract,
+               "dd bt val%d" % i, "tmp%d" % i, A.subtract)
+            for k in ((i - 1, i) if i % 2 else ()):
+                op("v", lambda: V.tensor_reduce(T.val[:, k + 2:k + 3], T.tmp[:, 8 * k:8 * k + 8], AxisListType.X, A.min,
+                                                apply_absolute_value=True), "tmp%d" % k, "val%d" % (k + 2))
+            if i == 3:
+                vt(wk[:, 0:16], T.bt[:, 0:256:17], T.nb[:], A.mult, "bt nb", "b2")
+            if i == 5:
+                vt(wk[:, 16:32], wk[:, 0:16], T.am[:], A.add, "b2 am", "b3")
+        if t == 0:
+            table_part(0)
+        vt(wk[:, 32:48], T.val[:], T.norm[:], A.mult, "norm0 norm1 " + " ".join("val%d" % i for i in range(16)), "t1")
+        vt(wk[:, 48:64], wk[:, 32:48], wk[:, 16:32], A.add, "t1 b3", "t2")
+        vt(wk[:, 64:80], wk[:, 48:64], T.yi[:], A.min, "t2 yi", "t3")
+        vc(T.ou[:], wk[:, 64:80], "t3", "ou")
+        vc(T.nu[:], T.nw[:].indirect(T.ou[:]), "nw0 nw1 nw2 nw3 nwi ou", "nu")
+        dmas("dgl" + ts, [("ys"[k % 2], gl[16 * k:16 * k + 16, :], T.nu[2 * k:128:16, 32 * k:32 * k + 32]) for k in range(8)], "nu", "gl" + ts)
+        if t < R - 1:
+            co = T["co" + ts]
+            ac(T.nbf[:], T.nw[:].indirect(T.ou[:]), "nw0 nw1 nw2 nw3 nwi ou", "nbf")
+            turn(T.at[:], T.nbf[:], "nbf", "at")
+            vc(co[:], T.at[:, 0:256:17], "at", "co" + ts)
+            send(T["ca" + ts][:], co[:], "rl" + ts, "ll" + ts, "co" + ts, "ca" + ts)
+            if t == 0:
+                vs(k0[:, 40:41], T.ip[:, 0:1], 8, None, A.bitwise_and, "ip", "k0m")
+                vs(kf[:, 56:57], k0[:, 40:41], 0.0, None, A.is_equal, "k0m", "mlo")
+                vs(kf[:, 57:58], k0[:, 40:41], 0.0, None, A.is_gt, "k0m", "mhi")
+            vs(wk[:, 80:96], co[:], kf[:, 56:57], None, A.mult, "mlo co" + ts, "m1")
+        for h in (1, 0):
+            k = "lh"[h] + ts
+            z, q, qs = T["z" + k], T["q" + k], T["q" + "lh"[h] + "s" + ts]
+            off = gl[:, 8 * h:8 * h + 8]
+            for b in range(4):
+                (vc if b < 2 else ac)(z[:, b:512:4], f[:, 256 * b:256 * b + 256].indirect(off), "f%d_%d gl%d" % (t, b, t), "z%s_%d" % (k, b))
+            quant(q[:], qs[:], z[:], " ".join("z%s_%d" % (k, b) for b in range(4)), "q" + k)
+            if h:
+                send(T["qa" + ts][:].bitcast(dt.uint8), q[:].bitcast(dt.uint8), "rc" + ts, "lc" + ts, "q" + k, "qac" + ts)
+                send(T["qas" + ts][:], qs[:], "rs" + ts, "ls" + ts, "q" + k, "qas" + ts)
+                if t == R - 1:
+                    send(T.ga[:], gl[:, 8:16], "rl" + ts, "ll" + ts, "gl" + ts, "ga")
+        if t < R - 1:
+            vs(wk[:, 96:112], T["ca" + ts][:], kf[:, 57:58], None, A.mult, "mhi ca" + ts, "m2")
+            vt(wk[:, 32:48], wk[:, 80:96], wk[:, 96:112], A.add, "m1 m2", "t1")
+            vc(T.lb[:, 0:16], wk[:, 32:48], "t1", "lb0 lb1")
+            prefetch_pick()
+            prefetch_rest()
+        else:
+            quant(T.qv[:], T.qvs[:], T.vt[:], "vt", "qv")
+
+        for h in (0, 1):
+            kk = "qac%d qas%d" % (t, t) if h else "ql" + ts
+            q, qs = T["q" + "la"[h] + ts], T["q" + "la"[h] + "s" + ts]
+            xk = "x%s%d" % ("lh"[h], t + 1)
+            x = T[xk]
+            for b in range(4):
+                a = slice(128 * b, 128 * b + 128)
+                mm(BANK[4 * h + b], 128, T.lw[:, a], T.lws[:, a], q[:], qs[:], "lw " + kk, True, False)
+                mm(BANK[4 * h + b], 128, T.qe[:, a], T.qes[:, a], q[:], qs[:], "qe " + kk, False, True)
+            for b in range(4):
+                bank = BANK[4 * h + b]
+                o, i, w = x[:, b:512:4], T[bank][:, 0:128], "%s_%d" % (xk, b)
+                if b % 2 == 0:
+                    vs(o, i, 0.015625, None, A.mult, bank, w)
+                else:
+                    ac(o, i, bank, w, 0.015625)
+            a = slice(128 * h, 128 * h + 128)
+            qn, qns = T["qx%d" % (t + 1)], T["qxs%d" % (t + 1)]
+            key = "qx%d%s" % (t + 1, "LH"[h])
+            quant(qn[:, a], qns[:, a], x[:], " ".join("%s_%d" % (xk, b) for b in range(4)), key)
+            if t < R - 1:
+                score_mm(t + 1, h)
+                score_bits(h)
+                continue
+            mm(BANK[h], 128, T.qv[:], T.qvs[:], qn[:, a], qns[:, a], "qv " + key)
+            lst = [("y", T.oc[:, 512 * h:512 * h + 512], qn[:, a].bitcast(dt.uint8))]
+            lst += [("y", T.osc[4 * k:4 * k + 4, a], qns[32 * k:32 * k + 4, a]) for k in range(4)]
+            dmas("doc" + "lh"[h], lst, key, "")
+            ac(T.oaf[:, a], T.nw[:, 2048:2304].indirect(T.ga[:] if h else gl[:, 0:8]), "nwi " + ("ga" if h else "gl" + ts), "oa%d" % h)
+            ac(T.ys[:, a], T[BANK[h]][:, 0:128], BANK[h], "ys%d" % h)
+            dmas("dy" + "lh"[h], [("s", T.y[:, a], T.ys[:, a])], "ys%d" % h, "")
+    dmas("doa", [("y", T.oa[:], T.oaf[0:128:16, :])], "oa0 oa1", "")
+    for s in sorted(cnt):
+        if known["g"].get(s, 0) < cnt[s]:
+            g.wait_ge(T.sem[s], cnt[s])

@@ -1,14 +1,14 @@
 from concourse.mybir import dt, AluOpType, AxisListType, ActivationFunctionType
 
 A = AluOpType
-COPY = ActivationFunctionType.Copy
+AF = ActivationFunctionType
 R = 3
 SCRATCH = {}
 for _d, _l in (
         ("int32", "nx4:512 ep:512 e8:128 ep2:256 pp:128 ai0:128 ai:128 n4i:512 sl:256 slt:256 ip:8 iph:8 iy:2 k0:64 pc:32 ei:128 am:16"),
-        ("float32", "p4:128 pr:256 pw:256 nw:2304 kf:64 mi:16 tb:16 oh:16 sc:1 cst:32 geo:32 ss:128 key:128 norm:16 nb:16 pg:256 pt:256 "
-                    "ek:128 dd:128 yi:16 tmp:128 wk:112 oaf:256 ys:256"),
-        ("bfloat16", "n4:512 nr:2048 i64:128 c64:128 et:2048 ut:512 vt:512 sb:256 bg:288 bt:288 nbf:256 at:256 val:16 f0:1024 f1:1024 "
+        ("float32", "p4:128 pr:256 pw:256 nw:2304 kf:64 cst:32 geo:32 ss:128 key:128 norm:16 c8:16 pg:256 pt:256 "
+                    "ek:128 dd:128 yi:16 amc:16 tmp:128 jk:128 wk:112 bg:288 bt:288 val:16 oaf:256 ys:256"),
+        ("bfloat16", "n4:512 nr:2048 i64:128 c64:128 et:2048 ut:512 vt:512 sb:256 nbf:256 at:256 f0:1024 f1:1024 "
                      "f2:1024 co0:16 co1:16 ca0:16 ca1:16 xl0:512 xl1:512 xl2:512 xl3:512 xh0:512 xh1:512 xh2:512 xh3:512 "
                      "zl0:512 zl1:512 zl2:512 zh0:512 zh1:512 zh2:512"),
         ("uint16", "ul:8 lb:18 ou:16 nu:256 ga:8 gl0:16 gl1:16 gl2:16")):
@@ -109,9 +109,9 @@ def rank_program(g, core, T, topo):
 
     def ac(out, i, r, w, scale=None):
         if scale is None:
-            op("s", lambda: S.activation(out, i, COPY), r, w)
+            op("s", lambda: S.activation(out, i, AF.Copy), r, w)
         else:
-            op("s", lambda: S.activation(out, i, COPY, scale=scale), r, w)
+            op("s", lambda: S.activation(out, i, AF.Copy, scale=scale), r, w)
 
     def fill(ap, c, w):
         op("v", lambda: V.memset(ap, c), "", w)
@@ -122,11 +122,14 @@ def rank_program(g, core, T, topo):
     def turn(o, i, r, w):
         op("v", lambda: V.transpose(o, i), r, w)
 
-    def iota(o, pat, cm, w, small=False):
+    def scan(o, d, first, r, w):
+        op("v", lambda: V.tensor_tensor_scan(o, d, T.cst[:, 16:24], first, A.mult, A.add), r, w)
+
+    def iota(o, pat, base, cm, w, small=False):
         if small:
-            op("g", lambda: g.iota(o, pat, 0, cm, allow_small_or_imprecise_dtypes=True), "", w)
+            op("g", lambda: g.iota(o, pat, base, cm, allow_small_or_imprecise_dtypes=True), "", w)
         else:
-            op("g", lambda: g.iota(o, pat, 0, cm), "", w)
+            op("g", lambda: g.iota(o, pat, base, cm), "", w)
 
     def mm(bank, n, l, ls, rh, rs, r, start=True, stop=True):
         op("t", lambda: P.matmul_mx(T[bank][:, 0:n], l, ls, rh, rs, start, stop), r, bank)
@@ -141,38 +144,43 @@ def rank_program(g, core, T, topo):
     dmas("dw", [("y", T.lw[:].bitcast(dt.uint8), T.wc[:]), ("s", T.lws[:], T.ws[:])], "", "lw")
     dmas("dv", [("y", T.vt[:], T.v[:])], "", "vt")
 
-    iota(T.ip[:], [[0, 8]], 1, "ip")
-    iota(T.ai0[0:32, :], [[0, 2], [4, 64]], 0, "ai0")
-    iota(T.iph[:], [[1, 8]], 1, "iph")
-    iota(T.iy[:], [[2, 2]], 16, "iy")
-    iota(T.mi[:], [[1, 16]], 0, "mi", True)
+    iota(T.ip[:], [[0, 8]], 0, 1, "ip")
+    iota(T.ai0[0:32, :], [[0, 2], [4, 64]], 0, 0, "ai0")
+    iota(T.iph[:], [[1, 8]], 0, 1, "iph")
+    iota(T.iy[:], [[2, 2]], 0, 16, "iy")
     op("g", lambda: g.affine_select(T.i64[:], T.c64[:], [[-1, 128]], A.is_equal, 0.0, 0, 1), "c64", "i64")
-    iota(T.key[:], [[16, 4], [256, 2], [0, 16]], 0, "key", True)
-    iota(T.et[:], [[0, 2048]], 0, "et", True)
-    iota(T.nw[:, 2048:2304], [[1, 256]], 0, "nwi", True)
+    iota(T.c8[:], [[0, 8], [64, 2]], -19, 0, "c8i", True)
+    iota(T.et[:], [[0, 2048]], 0, 0, "et", True)
+    for e in range(4):
+        iota(T.key[:, 32 * e:32 * e + 16], [[0, 8], [512, 2]], -31 - 32 * e, 0, "key%d" % e, True)
+        iota(T.key[:, 32 * e + 16:32 * e + 32], [[0, 8], [-512, 2]], 33 + 32 * e, 0, "key%d" % (e + 4), True)
+    iota(T.nw[:, 2048:2304], [[1, 256]], 0, 0, "nwi", True)
 
-    fill(T.cst[:, 0:8], 0.0625, "cst0")
-    fill(T.cst[:, 8:16], 16.0, "cst1")
+    fill(T.cst[:, 0:8], 2.0 ** -5, "cst0")
+    fill(T.cst[:, 8:16], 32.0, "cst1")
     fill(T.cst[:, 16:24], 0.0, "cst2")
-    fill(T.tb[:], 0.0, "tb")
     vs(k0[:, 0:1], T.ip[:, 0:1], 3, None, A.bitwise_and, "ip", "k0a")
+    scan(T.geo[:, 0:8], T.cst[:, 0:8], 64.0, "cst0 cst2", "geo0")
+    scan(T.geo[:, 8:16], T.cst[:, 8:16], 2.0 ** -9, "cst1 cst2", "geo1")
     vc(kf[:, 0:1], k0[:, 0:1], "k0a", "kfa")
-    vs(T.ai[0:32, :], T.ai0[0:32, :], kf[0:32, 0:1], 65536.0, A.add, "ai0 kfa", "aix", A.mult)
-    vs(T.ai[0:32, :], T.ai[0:32, :], 7 * 4369.0, None, A.add, "aix", "ai")
     vs(k0[:, 8:16], T.ip[:], 14, None, A.bitwise_and, "ip", "k0b")
-    vs(k0[:, 16:17], T.ip[:, 0:1], 4, 1, A.logical_shift_right, "ip", "k0d", A.bitwise_and)
+    for y in range(2):
+        vc(T.ss[:, y:16:2], T.geo[:, 0:8], "geo0", "ss%d" % y)
     vs(k0[:, 24:32], T.iph[:], 1, None, A.bitwise_and, "iph", "k0c")
     vs(kf[:, 8:16], k0[:, 8:16], 8.0, None, A.mult, "k0b", "kfb")
+    vs(T.ai[0:32, :], T.ai0[0:32, :], kf[0:32, 0:1], 65536.0, A.add, "ai0 kfa", "aix", A.mult)
+    vc(T.ss[:, 16:32], T.ss[:, 0:16], "ss0 ss1", "ss2")
     vt(kf[:, 16:24], kf[:, 8:16], k0[:, 24:32], A.add, "kfb k0c", "kfc")
+    vs(T.ai[0:32, :], T.ai[0:32, :], 7 * 4369.0, None, A.add, "aix", "ai")
+    vc(T.ss[:, 32:64], T.ss[:, 0:32], "ss0 ss1 ss2", "ss3")
     vc(T.ul[:], kf[:, 16:24], "kfc", "ul")
-    op("v", lambda: V.tensor_tensor_scan(T.geo[:, 0:8], T.cst[:, 0:8], T.cst[:, 16:24], 4096.0, A.mult, A.add), "cst0 cst2", "geo0")
 
+    vs(T.e8[0:32, :], T.nx4[0:32, 384:512], 8.0, None, A.mult, "nx4", "e8")
     for e in range(4):
         a = slice(128 * e, 128 * e + 128)
         if e < 3:
             vs(T.ep[0:32, a], T.nx4[0:32, a], 9 - 4 * e, 7 << (4 * e), A.logical_shift_right, "nx4", "ep%d" % e, A.bitwise_and)
         else:
-            vs(T.e8[0:32, :], T.nx4[0:32, a], 8.0, None, A.mult, "nx4", "e8")
             vs(T.ep[0:32, a], T.e8[0:32, :], 7 << 12, None, A.bitwise_and, "e8", "ep3")
     vt(T.ep2[0:32, :], T.ep[0:32, 0:256], T.ep[0:32, 256:512], A.add, "ep0 ep1 ep2 ep3", "epx")
     vt(T.pp[0:32, :], T.ep2[0:32, 0:128], T.ep2[0:32, 128:256], A.add, "epx", "pp")
@@ -186,117 +194,136 @@ def rank_program(g, core, T, topo):
     vs(T.n4i[0:32, :], T.nx4[0:32, :], 511, None, A.bitwise_and, "nx4", "n4i")
     vc(T.n4[0:32, :], T.n4i[0:32, :], "n4i", "n4")
     dmas("dnr", [("sy"[z], T.nr[16 * H + z:16 * H + 16:2, :], T.n4[0:32, :]) for H in range(8) for z in range(2)], "n4", "nr")
-
-    turn(T.slt[:], T.sl[:], "sl", "slt")
-    vc(T.lb[:, 0:16:2], T.slt[:, 0:256:34], "slt", "lb0")
-    vc(T.lb[:, 1:16:2], T.slt[:, 16:256:34], "slt", "lb1")
-    quant(T.qu[:], T.qus[:], T.ut[:], "ut", "qu")
-    vc(T.qy[:].bitcast(dt.uint32), T.qu[:].bitcast(dt.uint32).indirect(T.ul[:]), "qu ul", "qy")
-    ac(T.qys[:], T.qus[:].indirect(T.ul[:]), "qu ul", "qys")
-    quant(T.qx0[:, 0:128], T.qxs0[:, 0:128], T.xl0[:], "xl0", "qx0L")
-    quant(T.qx0[:, 128:256], T.qxs0[:, 128:256], T.xh0[:], "xh0", "qx0H")
-    for r in range(4):
-        vc(T.pw[:, r:256:4], T.pr[:, 64 * r:64 * r + 64], "pr", "pw%d" % r)
-
-    def prefetch_pick():
-        ac(T.pg[:], T.pw[:].indirect(T.lb[:, 0:16]), "pw0 pw1 pw2 pw3 lb0 lb1", "pg")
-
-    prefetch_pick()
-    fill(T.tb[:, 1:2], 32.0, "tb")
-    fill(T.tb[:, 3:4], 16.0, "tb")
-    vc(T.tb[:, 0:16:2], T.geo[:, 0:8], "geo0", "tb")
-    vt(kf[:, 49:50], k0[:, 24:25], k0[:, 16:17], A.not_equal, "k0c k0d", "kfh")
-    vt(kf[:, 50:51], k0[:, 8:9], kf[:, 49:50], A.add, "k0b kfh", "kfi")
-    vs(T.oh[:], T.mi[:], kf[:, 50:51], None, A.is_equal, "mi kfi", "oh")
-    vt(T.oh[:], T.oh[:], T.tb[:], A.mult, "oh tb", "oh")
-    op("v", lambda: V.tensor_reduce(T.sc[:], T.oh[:], AxisListType.X, A.add), "oh", "sc")
-    for y in range(2):
-        vs(T.ss[:, y:16:2], T.geo[:, 0:8], 2.0 ** -8, None, A.mult, "geo0", "ss%d" % y)
-    vc(T.ss[:, 16:32], T.ss[:, 0:16], "ss0 ss1", "ss2")
-    vc(T.ss[:, 32:64], T.ss[:, 0:32], "ss0 ss1 ss2", "ss3")
-    vc(T.ss[:, 64:128], T.ss[:, 0:64], "ss0 ss1 ss2 ss3", "ss4")
     for b in range(4):
         ac(T.et[:, 512 * b + b:512 * b + 512:4], T.i64[:], "i64 et", "et_%d" % b)
-
-    def prefetch_rest():
-        turn(T.pt[:], T.pg[:], "pg", "pt")
-        vc(T.pc[:, 0:16], T.pt[:, 0:256:17], "pt", "pc0")
-        vc(T.pc[:, 16:32:2], T.pt[:, 1:256:34], "pt", "pc1")
-        vc(T.pc[:, 17:32:2], T.pt[:, 16:256:34], "pt", "pc2")
-        for e in range(4):
-            vs(T.ei[:, 32 * e:32 * e + 32], T.pc[:], 4 * e, 7, A.logical_shift_right, "pc0 pc1 pc2", "ei%d" % e, A.bitwise_and)
-        vt(T.ek[:], T.ei[:], T.key[:], A.add, "ei0 ei1 ei2 ei3 key", "ek")
-        vt(T.dd[:], T.ek[:], T.ss[:], A.mult, "ek ss0 ss1 ss2 ss3 ss4", "dd")
-        vs(T.am[:], T.pc[:, 0:16], 16, None, A.logical_shift_right, "pc0", "am")
-        vs(T.yi[:], T.am[:], 2048.0, None, A.add, "am", "yi")
-
-    def table_part(r):
-        (ac if r else vc)(T.nw[:, r:2048:4], T.nr[:, 512 * r:512 * r + 512], "nr", "nw%d" % r)
 
     def score_mm(t, h):
         a = slice(128 * h, 128 * h + 128)
         mm(BANK[h], 128, T.qy[:], T.qys[:], T["qx%d" % t][:, a], T["qxs%d" % t][:, a], "qy qys qx%d" % t + "LH"[h])
 
     def score_bits(h):
-        vs(T.sb[:, 128 * h:128 * h + 128], T[BANK[h]][:, 0:128], 0.0, T.sc[:], A.is_gt, BANK[h] + " sc", "sb%d" % h, A.mult)
+        vs(T.sb[:, 128 * h:128 * h + 128], T[BANK[h]][:, 0:128], 0.0, 0.5, A.is_gt, BANK[h], "sb%d" % h, A.subtract)
 
-    def unpack(t):
-        for b in range(4):
-            a = slice(128 * b, 128 * b + 128)
-            mm(BANK[2 + b], 256, T.qe[:, a], T.qes[:, a], T["qx%d" % t][:], T["qxs%d" % t][:], "qe qx%dL qx%dH" % (t, t))
-        for b in range(4):
-            ac(T["f%d" % t][:, 256 * b:256 * b + 256], T[BANK[2 + b]][:, 0:256], BANK[2 + b], "f%d_%d" % (t, b), 0.015625)
-
+    quant(T.qu[:], T.qus[:], T.ut[:], "ut", "qu")
+    turn(T.slt[:], T.sl[:], "sl", "slt")
+    vc(T.qy[:].bitcast(dt.uint32), T.qu[:].bitcast(dt.uint32).indirect(T.ul[:]), "qu ul", "qy")
+    ac(T.qys[:], T.qus[:].indirect(T.ul[:]), "qu ul", "qys")
+    quant(T.qx0[:, 0:128], T.qxs0[:, 0:128], T.xl0[:], "xl0", "qx0L")
+    quant(T.qx0[:, 128:256], T.qxs0[:, 128:256], T.xh0[:], "xh0", "qx0H")
     score_mm(0, 0)
     score_mm(0, 1)
     vs(k0[:, 32:34], T.ip[:, 0:2], 4, None, A.logical_shift_right, "ip", "k0e")
+    vc(T.lb[:, 0:16:2], T.slt[:, 0:256:34], "slt", "lb0")
+    vc(T.lb[:, 1:16:2], T.slt[:, 16:256:34], "slt", "lb1")
+    vs(k0[:, 16:17], k0[:, 32:33], 1, None, A.bitwise_and, "k0e", "k0d")
     vs(kf[:, 32:34], k0[:, 32:34], -254.0, None, A.mult, "k0e", "kfe")
-    vt(kf[:, 34:36], kf[:, 32:34], T.iy[:], A.add, "kfe iy", "kff")
+    vs(T.c8[:], T.c8[:], 0.5, None, A.mult, "c8i", "c8")
     vc(kf[:, 40:41], k0[:, 16:17], "k0d", "kfd")
+    vt(kf[:, 34:36], kf[:, 32:34], T.iy[:], A.add, "kfe iy", "kff")
+    vc(T.ss[:, 64:128], T.ss[:, 0:64], "ss0 ss1 ss2 ss3", "ss4")
     vs(T.lb[:, 16:18], kf[:, 34:36], kf[:, 40:41], None, A.subtract, "kff kfd", "lbj")
     score_bits(0)
     score_bits(1)
+    vc(T.norm[:, 0:16:2], T.geo[:, 8:16], "geo1", "norm0")
+    vs(T.norm[:, 1:16:2], T.geo[:, 8:16], -1.0, None, A.mult, "geo1", "norm1")
+    for r in range(4):
+        (ac if r % 2 else vc)(T.pw[:, r:256:4], T.pr[:, 64 * r:64 * r + 64], "pr", "pw%d" % r)
+
+    def prefetch_pick():
+        ac(T.pg[:], T.pw[:].indirect(T.lb[:, 0:16]), "pw0 pw1 pw2 pw3 lb0 lb1", "pg")
+
+    def prefetch_rest():
+        turn(T.pt[:], T.pg[:], "pg", "pt")
+        vc(T.pc[:, 0:16], T.pt[:, 0:256:17], "pt", "pc0")
+        vc(T.pc[:, 16:32:2], T.pt[:, 1:256:34], "pt", "pc1")
+        vc(T.pc[:, 17:32:2], T.pt[:, 16:256:34], "pt", "pc2")
+        vs(T.am[:], T.pc[:, 0:16], 16, None, A.logical_shift_right, "pc0", "am")
+        for e in range(4):
+            vs(T.ei[:, 32 * e:32 * e + 32], T.pc[:], 4 * e, 7, A.logical_shift_right, "pc0 pc1 pc2", "ei%d" % e, A.bitwise_and)
+        vs(T.yi[:], T.am[:], 2.0 ** -8, 8.0, A.mult, "am", "yi", A.add)
+        vt(T.ek[:], T.ei[:], T.key[:], A.add, "ei0 ei1 ei2 ei3 " + " ".join("key%d" % k for k in range(8)), "ek")
+        vt(T.amc[:], T.yi[:], T.c8[:], A.add, "yi c8", "amc")
+        vt(T.dd[:], T.ek[:], T.ss[:], A.mult, "ek ss0 ss1 ss2 ss3 ss4", "dd")
+
+    def bits_pick():
+        ac(T.bg[:, 160:288], T.sb[:].indirect(T.lb[:, 10:18]), "sb0 sb1 lb0 lb1 lbj", "bg1")
+        vc(T.bg[:, 0:160], T.sb[:].indirect(T.lb[:, 0:10]), "sb0 sb1 lb0 lb1", "bg0")
+
+    prefetch_pick()
+    bits_pick()
+    for r in range(4):
+        ac(T.nw[:, r:2048:4], T.nr[:, 512 * r:512 * r + 512], "nr", "nw%d" % r)
+    NW = "nw0 nw1 nw2 nw3 nwi "
     prefetch_rest()
 
+    bt, val, tmp = T.bt, T.val, T.tmp
     for t in range(R):
         ts = "%d" % t
         gl, f = T["gl" + ts], T["f" + ts]
-        vc(T.bg[:], T.sb[:].indirect(T.lb[:]), "sb0 sb1 lb0 lb1 lbj", "bg")
-        if t == 0:
-            for r in (1, 2, 3):
-                table_part(r)
-            quant(T.qe[:], T.qes[:], T.et[:], "et et_0 et_1 et_2 et_3", "qe")
-            op("v", lambda: V.tensor_tensor_scan(T.geo[:, 8:16], T.cst[:, 8:16], T.cst[:, 16:24], 2.0, A.mult, A.add), "cst1 cst2", "geo1")
-            for y in range(2):
-                vc(T.norm[:, y:16:2], T.geo[:, 8:16], "geo1", "norm%d" % y)
-            vs(T.nb[:], T.norm[:], 2.0 ** -5, None, A.mult, "norm0 norm1", "nb")
-        unpack(t)
-        turn(T.bt[:], T.bg[:], "bg", "bt")
-        vt(T.val[:, 0:2], T.bt[:, 257:273:15], T.bt[:, 259:275:15], A.add, "bt", "val0 val1")
+
+        def unpack():
+            for b in range(4):
+                a = slice(128 * b, 128 * b + 128)
+                mm(BANK[2 + b], 256, T.qe[:, a], T.qes[:, a], T["qx" + ts][:], T["qxs" + ts][:], "qe qx%dL qx%dH" % (t, t))
+
+        if t:
+            bits_pick()
+            unpack()
+        turn(bt[:, 256:288], T.bg[:, 256:288], "bg1", "bte")
+        vs(wk[:, 0:1], bt[:, 257:258], 64.0, 80.0, A.mult, "bte", "w0", A.add)
+        op("s", lambda: S.activation(wk[:, 8:9], bt[:, 272:273], AF.Identity, bias=432.0, scale=-64.0), "bte", "w1")
+        turn(bt[:, 0:256], T.bg[:, 0:256], "bg0 bg1", "bt")
+        vs(val[:, 0:1], bt[:, 259:260], 32.0, wk[:, 0:1], A.mult, "bte w0", "val0", A.add)
+        op("s", lambda: S.activation(val[:, 1:2], bt[:, 274:275], AF.Identity, bias=wk[:, 8:9], scale=-32.0), "bte w1", "val1")
+        x0, x1, x2, o = wk[:, 32:46], wk[:, 48:62], wk[:, 64:78], T.ou
+
+        def last(y):
+            i = 14 + y
+            vs(wk[:, 46 + y:47 + y], val[:, i:i + 1], (-1.0) ** y * 2.0 ** 31, wk[:, 16 + i:17 + i], A.mult, "val%d b3" % i, "l%d" % y, A.add)
+
+        def last2(y):
+            i = 14 + y
+            vs(o[:, i:i + 1], wk[:, 46 + y:47 + y], T.yi[:, i:i + 1], 256.0, A.min, "l%d yi" % y, "ou%d" % y, A.mult)
+
         for i in range(14):
-            vs(T.tmp[:, 8 * i:8 * i + 8], T.dd[:, i:128:16], T.val[:, i:i + 1], T.bt[:, 17 * i:17 * i + 1], A.subtract,
-               "dd bt val%d" % i, "tmp%d" % i, A.subtract)
-            for k in ((i - 1, i) if i % 2 else ()):
-                op("v", lambda: V.tensor_reduce(T.val[:, k + 2:k + 3], T.tmp[:, 8 * k:8 * k + 8], AxisListType.X, A.min,
-                                                apply_absolute_value=True), "tmp%d" % k, "val%d" % (k + 2))
-            if i == 3:
-                vt(wk[:, 0:16], T.bt[:, 0:256:17], T.nb[:], A.mult, "bt nb", "b2")
-            if i == 5:
-                vt(wk[:, 16:32], wk[:, 0:16], T.am[:], A.add, "b2 am", "b3")
-        if t == 0:
-            table_part(0)
-        vt(wk[:, 32:48], T.val[:], T.norm[:], A.mult, "norm0 norm1 " + " ".join("val%d" % i for i in range(16)), "t1")
-        vt(wk[:, 48:64], wk[:, 32:48], wk[:, 16:32], A.add, "t1 b3", "t2")
-        vt(wk[:, 64:80], wk[:, 48:64], T.yi[:], A.min, "t2 yi", "t3")
-        vc(T.ou[:], wk[:, 64:80], "t3", "ou")
-        vc(T.nu[:], T.nw[:].indirect(T.ou[:]), "nw0 nw1 nw2 nw3 nwi ou", "nu")
+            c, d = slice(8 * i, 8 * i + 8), T.dd[:, i:128:16]
+            me, sg, new = val[:, i:i + 1], bt[:, 17 * i:17 * i + 1], val[:, i + 2:i + 3]
+            if i % 2:
+                op("s", lambda: S.activation(tmp[:, c], d, AF.Abs, bias=me, scale=sg), "dd bt val%d" % i, "tmp%d" % i)
+                op("s", lambda: S.activation(T.jk[:, c], tmp[:, c], AF.Relu, bias=16.0 * 32.0 ** -(i // 2), scale=-1.0, accum_out=new),
+                   "tmp%d" % i, "jk%d val%d" % (i, i + 2))
+            else:
+                vs(tmp[:, c], d, sg, me, A.mult, "dd bt val%d" % i, "tmp%d" % i, A.subtract)
+                if i == 2:
+                    vt(wk[:, 16:32], bt[:, 0:256:17], T.amc[:], A.add, "bt amc", "b3")
+                op("v", lambda: V.tensor_reduce(new, tmp[:, c], AxisListType.X, A.min, apply_absolute_value=True), "tmp%d" % i, "val%d" % (i + 2))
+        vt(x0, val[:, 0:14], T.norm[:, 0:14], A.mult, "norm0 norm1 " + " ".join("val%d" % i for i in range(14)), "t1")
+        last(0)
+        vt(x1, x0, wk[:, 16:30], A.add, "t1 b3", "t2")
+        last2(0)
+        vt(x2, x1, T.yi[:, 0:14], A.min, "t2 yi", "t3")
+        last(1)
+        vs(o[:, 0:14], x2, 256.0, None, A.mult, "t3", "ou")
+        last2(1)
+        vc(T.nu[:], T.nw[:].indirect(o[:]), NW + "ou ou0 ou1", "nu")
+        if t < R - 1:
+            ac(T.nbf[:], T.nw[:].indirect(o[:]), NW + "ou ou0 ou1", "nbf")
         dmas("dgl" + ts, [("ys"[k % 2], gl[16 * k:16 * k + 16, :], T.nu[2 * k:128:16, 32 * k:32 * k + 32]) for k in range(8)], "nu", "gl" + ts)
         if t < R - 1:
             co = T["co" + ts]
-            ac(T.nbf[:], T.nw[:].indirect(T.ou[:]), "nw0 nw1 nw2 nw3 nwi ou", "nbf")
             turn(T.at[:], T.nbf[:], "nbf", "at")
             vc(co[:], T.at[:, 0:256:17], "at", "co" + ts)
             send(T["ca" + ts][:], co[:], "rl" + ts, "ll" + ts, "co" + ts, "ca" + ts)
+        if t == 0:
+            quant(T.qe[:], T.qes[:], T.et[:], "et et_0 et_1 et_2 et_3", "qe")
+            unpack()
+        for b in range(4):
+            o, i = f[:, 256 * b:256 * b + 256], T[BANK[2 + b]][:, 0:256]
+            if b % 2:
+                vs(o, i, 0.015625, None, A.mult, BANK[2 + b], "f%d_%d" % (t, b))
+            else:
+                ac(o, i, BANK[2 + b], "f%d_%d" % (t, b), 0.015625)
+        if t < R - 1:
             if t == 0:
                 vs(k0[:, 40:41], T.ip[:, 0:1], 8, None, A.bitwise_and, "ip", "k0m")
                 vs(kf[:, 56:57], k0[:, 40:41], 0.0, None, A.is_equal, "k0m", "mlo")
@@ -316,7 +343,7 @@ def rank_program(g, core, T, topo):
                     send(T.ga[:], gl[:, 8:16], "rl" + ts, "ll" + ts, "gl" + ts, "ga")
         if t < R - 1:
             vs(wk[:, 96:112], T["ca" + ts][:], kf[:, 57:58], None, A.mult, "mhi ca" + ts, "m2")
-            vt(wk[:, 32:48], wk[:, 80:96], wk[:, 96:112], A.add, "m1 m2", "t1")
+            vt(wk[:, 32:48], wk[:, 80:96], wk[:, 96:112], A.add, "m1 m2", "t1 l0 l1")
             vc(T.lb[:, 0:16], wk[:, 32:48], "t1", "lb0 lb1")
             prefetch_pick()
             prefetch_rest()
@@ -335,7 +362,7 @@ def rank_program(g, core, T, topo):
             for b in range(4):
                 bank = BANK[4 * h + b]
                 o, i, w = x[:, b:512:4], T[bank][:, 0:128], "%s_%d" % (xk, b)
-                if b % 2 == 0:
+                if b % 2:
                     vs(o, i, 0.015625, None, A.mult, bank, w)
                 else:
                     ac(o, i, bank, w, 0.015625)

@@ -8,13 +8,13 @@ for _d, _l in (
         ("int32", "nx4:512 ep:512 e8:128 ep2:256 pp:128 ai0:128 ai:128 n4i:512 sl:256 slt:256 ip:8 iph:8 iy:2 k0:64 pc:32 ei:128 am:16"),
         ("float32", "p4:128 pr:256 pw:256 nw:2304 kf:64 cst:32 geo:32 ss:128 key:128 norm:16 c8:16 pg:256 pt:256 "
                     "ek:128 dd:128 yi:16 amc:16 tmp:128 jk:128 wk:112 bg:288 bt:288 val:16 oaf:256 ys:256"),
-        ("bfloat16", "n4:512 nr:2048 i64:128 c64:128 et:2048 ut:512 vt:512 sb:256 nbf:256 at:256 f0:1024 f1:1024 "
-                     "f2:1024 co0:16 co1:16 ca0:16 ca1:16 xl0:512 xl1:512 xl2:512 xl3:512 xh0:512 xh1:512 xh2:512 xh3:512 "
+        ("bfloat16", "n4:512 nr:2048 i64:128 c64:128 et:2048 ut:512 vt:512 sb:256 nbf:256 at:256 f:1024 fa:1024 "
+                     "co0:16 co1:16 ca0:16 ca1:16 xl0:512 xl1:512 xl2:512 xl3:512 xh0:512 xh1:512 xh2:512 xh3:512 "
                      "zl0:512 zl1:512 zl2:512 zh0:512 zh1:512 zh2:512"),
-        ("uint16", "ul:8 lb:18 ou:16 nu:256 ga:8 gl0:16 gl1:16 gl2:16")):
+        ("uint16", "ul:8 lb:18 ou:16 nu:256 ga0:8 ga1:8 ga2:8 gl0:16 gl1:16 gl2:16")):
     for _s in _l.split():
         SCRATCH[_s.split(":")[0]] = ("sbuf", [128, int(_s.split(":")[1])], _d)
-for _s in "qe:512 lw:512 qu:128 qy:128 qv:128 qx:256:4 qh:128:3 ql:128:3 qa:128:3".split():
+for _s in "qe:512 lw:512 qu:128 qy:128 qv:128 qx:256:4 qh:128:3 ql:128:3 qn:256:3".split():
     _p = _s.split(":")
     for _t in ([""] if len(_p) == 2 else ["%d" % k for k in range(int(_p[2]))]):
         SCRATCH[_p[0] + _t] = ("sbuf", [128, int(_p[1])], "float8_e4m3fn_x4")
@@ -23,7 +23,7 @@ BANK = ["b%d" % k for k in range(10, 18)]
 for _s in BANK:
     SCRATCH[_s] = ("psum", [128, 512], "float32")
 SEMAPHORES = ("cv cs ct cg dnx dal dx du dv dw dpr dnr dyl dyh doa docl doch dgl0 dgl1 dgl2".split()
-              + [n + "%d" % t for n in ("rl", "ll", "rc", "lc", "rs", "ls") for t in range(R)])
+              + [n + "%d" % t for n in ("rl", "ll", "rc", "lc", "rs", "ls", "rg", "lg") for t in range(R)])
 
 
 def rank_program(g, core, T, topo):
@@ -62,7 +62,7 @@ def rank_program(g, core, T, topo):
             wr[k] = tok
             rd[k] = []
 
-    def op(q, fn, r, w):
+    def op(q, fn, r, w, more=""):
         r, w = r.split(), w.split()
         w = w + [k for k in r if k in BANK]
         deps(q, r, w)
@@ -71,7 +71,7 @@ def rank_program(g, core, T, topo):
         fn().then_inc(T.sem[s], 1)
         clk = dict(known[q])
         clk[s] = cnt[s]
-        note((s, cnt[s], clk), r, w)
+        note((s, cnt[s], clk), r, w + more.split())
 
     def dmas(sem, lst, r, w):
         r, w = r.split(), w.split()
@@ -87,12 +87,13 @@ def rank_program(g, core, T, topo):
                 clk[s] = max(clk.get(s, 0), n)
         note((sem, cnt[sem], clk), r, w)
 
-    def send(out, inp, rs, ls, r, lands):
-        deps("g", [r], [])
+    def send(out, inp, k, t, r, lands):
+        rs, ls, r = "r%s%d" % (k, t), "l%s%d" % (k, t), r.split()
+        deps("g", r, [])
         g.remote_dma(out, inp, T.sem[rs], T.sem[ls], pid, rid, mask)
         for s in (ls, rs):
             cnt[s] = cnt.get(s, 0) + neng
-        note((ls, cnt[ls], {}), [r], [])
+        note((ls, cnt[ls], {}), r, [])
         note((rs, cnt[rs], {}), [], [lands])
 
     def vs(out, i, s1, s2, o1, r, w, o2=None):
@@ -132,7 +133,7 @@ def rank_program(g, core, T, topo):
             op("g", lambda: g.iota(o, pat, base, cm), "", w)
 
     def mm(bank, n, l, ls, rh, rs, r, start=True, stop=True):
-        op("t", lambda: P.matmul_mx(T[bank][:, 0:n], l, ls, rh, rs, start, stop), r, bank)
+        op("t", lambda: P.matmul_mx(T[bank][:, 0:n], l, ls, rh, rs, start, stop), r, bank if start else "", bank)
 
     k0, kf, wk = T.k0, T.kf, T.wk
     dmas("dnx", [("ys"[e // 2], T.nx4[0:32, 128 * e:128 * e + 128], T.nx[e:128:4, :]) for e in range(4)], "", "nx4")
@@ -154,7 +155,6 @@ def rank_program(g, core, T, topo):
     for e in range(4):
         iota(T.key[:, 32 * e:32 * e + 16], [[0, 8], [512, 2]], -31 - 32 * e, 0, "key%d" % e, True)
         iota(T.key[:, 32 * e + 16:32 * e + 32], [[0, 8], [-512, 2]], 33 + 32 * e, 0, "key%d" % (e + 4), True)
-    iota(T.nw[:, 2048:2304], [[1, 256]], 0, 0, "nwi", True)
 
     fill(T.cst[:, 0:8], 2.0 ** -5, "cst0")
     fill(T.cst[:, 8:16], 32.0, "cst1")
@@ -204,12 +204,19 @@ def rank_program(g, core, T, topo):
     def score_bits(h):
         vs(T.sb[:, 128 * h:128 * h + 128], T[BANK[h]][:, 0:128], 0.0, 0.5, A.is_gt, BANK[h], "sb%d" % h, A.subtract)
 
+    def send_state(t):
+        k = "qx%dL qx%dH" % (t, t)
+        send(T["qn%d" % t][:].bitcast(dt.uint8), T["qx%d" % t][:].bitcast(dt.uint8), "c", t, k, "qnc%d" % t)
+        send(T["qns%d" % t][:], T["qxs%d" % t][:], "s", t, k, "qns%d" % t)
+
     quant(T.qu[:], T.qus[:], T.ut[:], "ut", "qu")
     turn(T.slt[:], T.sl[:], "sl", "slt")
     vc(T.qy[:].bitcast(dt.uint32), T.qu[:].bitcast(dt.uint32).indirect(T.ul[:]), "qu ul", "qy")
     ac(T.qys[:], T.qus[:].indirect(T.ul[:]), "qu ul", "qys")
     quant(T.qx0[:, 0:128], T.qxs0[:, 0:128], T.xl0[:], "xl0", "qx0L")
     quant(T.qx0[:, 128:256], T.qxs0[:, 128:256], T.xh0[:], "xh0", "qx0H")
+    iota(T.nw[:, 2048:2304], [[1, 256]], 0, 0, "nwi", True)
+    send_state(0)
     score_mm(0, 0)
     score_mm(0, 1)
     vs(k0[:, 32:34], T.ip[:, 0:2], 4, None, A.logical_shift_right, "ip", "k0e")
@@ -232,11 +239,13 @@ def rank_program(g, core, T, topo):
     def prefetch_pick():
         ac(T.pg[:], T.pw[:].indirect(T.lb[:, 0:16]), "pw0 pw1 pw2 pw3 lb0 lb1", "pg")
 
-    def prefetch_rest():
+    def prefetch_1():
         turn(T.pt[:], T.pg[:], "pg", "pt")
         vc(T.pc[:, 0:16], T.pt[:, 0:256:17], "pt", "pc0")
         vc(T.pc[:, 16:32:2], T.pt[:, 1:256:34], "pt", "pc1")
         vc(T.pc[:, 17:32:2], T.pt[:, 16:256:34], "pt", "pc2")
+
+    def prefetch_2():
         vs(T.am[:], T.pc[:, 0:16], 16, None, A.logical_shift_right, "pc0", "am")
         for e in range(4):
             vs(T.ei[:, 32 * e:32 * e + 32], T.pc[:], 4 * e, 7, A.logical_shift_right, "pc0 pc1 pc2", "ei%d" % e, A.bitwise_and)
@@ -251,24 +260,24 @@ def rank_program(g, core, T, topo):
 
     prefetch_pick()
     bits_pick()
+    quant(T.qe[:], T.qes[:], T.et[:], "et et_0 et_1 et_2 et_3", "qe")
     for r in range(4):
         ac(T.nw[:, r:2048:4], T.nr[:, 512 * r:512 * r + 512], "nr", "nw%d" % r)
     NW = "nw0 nw1 nw2 nw3 nwi "
-    prefetch_rest()
+    prefetch_1()
+    prefetch_2()
 
     bt, val, tmp = T.bt, T.val, T.tmp
     for t in range(R):
         ts = "%d" % t
-        gl, f = T["gl" + ts], T["f" + ts]
-
-        def unpack():
-            for b in range(4):
-                a = slice(128 * b, 128 * b + 128)
-                mm(BANK[2 + b], 256, T.qe[:, a], T.qes[:, a], T["qx" + ts][:], T["qxs" + ts][:], "qe qx%dL qx%dH" % (t, t))
-
+        gl, ga = T["gl" + ts], T["ga" + ts]
+        halves = (("f", T.f, [2, 3, 4, 5], "qx", "qx%dL qx%dH" % (t, t)), ("fa", T.fa, [6, 7, 0, 1], "qn", "qnc%d qns%d" % (t, t)))
         if t:
             bits_pick()
-            unpack()
+        for _, _, bk, q, k in halves:
+            for b in range(4):
+                a = slice(128 * b, 128 * b + 128)
+                mm(BANK[bk[b]], 256, T.qe[:, a], T.qes[:, a], T[q + ts][:], T[q + "s" + ts][:], "qe " + k)
         turn(bt[:, 256:288], T.bg[:, 256:288], "bg1", "bte")
         vs(wk[:, 0:1], bt[:, 257:258], 64.0, 80.0, A.mult, "bte", "w0", A.add)
         op("s", lambda: S.activation(wk[:, 8:9], bt[:, 272:273], AF.Identity, bias=432.0, scale=-64.0), "bte", "w1")
@@ -313,74 +322,81 @@ def rank_program(g, core, T, topo):
             co = T["co" + ts]
             turn(T.at[:], T.nbf[:], "nbf", "at")
             vc(co[:], T.at[:, 0:256:17], "at", "co" + ts)
-            send(T["ca" + ts][:], co[:], "rl" + ts, "ll" + ts, "co" + ts, "ca" + ts)
-        if t == 0:
-            quant(T.qe[:], T.qes[:], T.et[:], "et et_0 et_1 et_2 et_3", "qe")
-            unpack()
-        for b in range(4):
-            o, i = f[:, 256 * b:256 * b + 256], T[BANK[2 + b]][:, 0:256]
-            if b % 2:
-                vs(o, i, 0.015625, None, A.mult, BANK[2 + b], "f%d_%d" % (t, b))
-            else:
-                ac(o, i, BANK[2 + b], "f%d_%d" % (t, b), 0.015625)
-        if t < R - 1:
-            if t == 0:
-                vs(k0[:, 40:41], T.ip[:, 0:1], 8, None, A.bitwise_and, "ip", "k0m")
-                vs(kf[:, 56:57], k0[:, 40:41], 0.0, None, A.is_equal, "k0m", "mlo")
-                vs(kf[:, 57:58], k0[:, 40:41], 0.0, None, A.is_gt, "k0m", "mhi")
-            vs(wk[:, 80:96], co[:], kf[:, 56:57], None, A.mult, "mlo co" + ts, "m1")
-        for h in (1, 0):
-            k = "lh"[h] + ts
-            z, q, qs = T["z" + k], T["q" + k], T["q" + "lh"[h] + "s" + ts]
-            off = gl[:, 8 * h:8 * h + 8]
+            send(T["ca" + ts][:], co[:], "l", t, "co" + ts, "ca" + ts)
+        send(ga[:], gl[:, 8:16], "g", t, "gl" + ts, "ga" + ts)
+        for n, f, bk, _, _ in halves:
             for b in range(4):
-                (vc if b < 2 else ac)(z[:, b:512:4], f[:, 256 * b:256 * b + 256].indirect(off), "f%d_%d gl%d" % (t, b, t), "z%s_%d" % (k, b))
-            quant(q[:], qs[:], z[:], " ".join("z%s_%d" % (k, b) for b in range(4)), "q" + k)
-            if h:
-                send(T["qa" + ts][:].bitcast(dt.uint8), q[:].bitcast(dt.uint8), "rc" + ts, "lc" + ts, "q" + k, "qac" + ts)
-                send(T["qas" + ts][:], qs[:], "rs" + ts, "ls" + ts, "q" + k, "qas" + ts)
-                if t == R - 1:
-                    send(T.ga[:], gl[:, 8:16], "rl" + ts, "ll" + ts, "gl" + ts, "ga")
+                bank = BANK[bk[b]]
+                fo, fi = f[:, 256 * b:256 * b + 256], T[bank][:, 0:256]
+                if b % 2:
+                    vs(fo, fi, 0.015625, None, A.mult, bank, "%s_%d" % (n, b))
+                else:
+                    ac(fo, fi, bank, "%s_%d" % (n, b), 0.015625)
+            if n == "f" and t < R - 1:
+                if t == 0:
+                    vs(k0[:, 40:41], T.ip[:, 0:1], 8, None, A.bitwise_and, "ip", "k0m")
+                    vs(kf[:, 56:57], k0[:, 40:41], 0.0, None, A.is_equal, "k0m", "mlo")
+                    vs(kf[:, 57:58], k0[:, 40:41], 0.0, None, A.is_gt, "k0m", "mhi")
+                vs(wk[:, 80:96], co[:], kf[:, 56:57], None, A.mult, "mlo co" + ts, "m1")
+
+        def make_z(h):
+            k, n, off, ok = "lh"[h] + ts, ("f", "fa")[h], (gl[:, 0:8], ga[:])[h], ("gl", "ga")[h] + ts
+            z = T["z" + k]
+            for b in range(4):
+                (vc if b < 2 else ac)(z[:, b:512:4], T[n][:, 256 * b:256 * b + 256].indirect(off), "%s_%d %s" % (n, b, ok), "z%s_%d" % (k, b))
+            quant(T["q" + k][:], T["q" + "lh"[h] + "s" + ts][:], z[:], " ".join("z%s_%d" % (k, b) for b in range(4)), "q" + k)
+
+        def make_r(h):
+            q, qs, kk = T["q" + "lh"[h] + ts], T["q" + "lh"[h] + "s" + ts], "q" + "lh"[h] + ts
+            for b in range(4):
+                a = slice(128 * b, 128 * b + 128)
+                mm(BANK[4 * h + b], 128, T.lw[:, a], T.lws[:, a], q[:], qs[:], "lw " + kk, True, False)
+                mm(BANK[4 * h + b], 128, T.qe[:, a], T.qes[:, a], q[:], qs[:], "qe " + kk, False, True)
+
+        def make_x(h):
+            a, xk = slice(128 * h, 128 * h + 128), "x%s%d" % ("lh"[h], t + 1)
+            for b in range(4):
+                bank = BANK[4 * h + b]
+                xo, xi, w = T[xk][:, b:512:4], T[bank][:, 0:128], "%s_%d" % (xk, b)
+                if b % 2:
+                    vs(xo, xi, 0.015625, None, A.mult, bank, w)
+                else:
+                    ac(xo, xi, bank, w, 0.015625)
+            qn, qns, key = T["qx%d" % (t + 1)], T["qxs%d" % (t + 1)], "qx%d%s" % (t + 1, "LH"[h])
+            quant(qn[:, a], qns[:, a], T[xk][:], " ".join("%s_%d" % (xk, b) for b in range(4)), key)
+            if t < R - 1:
+                score_mm(t + 1, h)
+                return
+            mm(BANK[h], 128, T.qv[:], T.qvs[:], qn[:, a], qns[:, a], "qv " + key)
+            lst = [("y", T.oc[:, 512 * h:512 * h + 512], qn[:, a].bitcast(dt.uint8))]
+            lst += [("y", T.osc[4 * k:4 * k + 4, a], qns[32 * k:32 * k + 4, a]) for k in range(4)]
+            dmas("doc" + "lh"[h], lst, key, "")
+            ac(T.oaf[:, a], T.nw[:, 2048:2304].indirect(ga[:] if h else gl[:, 0:8]), "nwi " + ("ga" if h else "gl") + ts, "oa%d" % h)
+            ac(T.ys[:, a], T[BANK[h]][:, 0:128], BANK[h], "ys%d" % h)
+            dmas("dy" + "lh"[h], [("s", T.y[:, a], T.ys[:, a])], "ys%d" % h, "")
+
+        make_z(0)
+        make_r(0)
         if t < R - 1:
             vs(wk[:, 96:112], T["ca" + ts][:], kf[:, 57:58], None, A.mult, "mhi ca" + ts, "m2")
             vt(wk[:, 32:48], wk[:, 80:96], wk[:, 96:112], A.add, "m1 m2", "t1 l0 l1")
             vc(T.lb[:, 0:16], wk[:, 32:48], "t1", "lb0 lb1")
             prefetch_pick()
-            prefetch_rest()
+            make_x(0)
+            prefetch_1()
+            make_z(1)
+            make_r(1)
+            score_bits(0)
+            prefetch_2()
+            make_x(1)
+            send_state(t + 1)
+            score_bits(1)
         else:
             quant(T.qv[:], T.qvs[:], T.vt[:], "vt", "qv")
-
-        for h in (0, 1):
-            kk = "qac%d qas%d" % (t, t) if h else "ql" + ts
-            q, qs = T["q" + "la"[h] + ts], T["q" + "la"[h] + "s" + ts]
-            xk = "x%s%d" % ("lh"[h], t + 1)
-            x = T[xk]
-            for b in range(4):
-                a = slice(128 * b, 128 * b + 128)
-                mm(BANK[4 * h + b], 128, T.lw[:, a], T.lws[:, a], q[:], qs[:], "lw " + kk, True, False)
-                mm(BANK[4 * h + b], 128, T.qe[:, a], T.qes[:, a], q[:], qs[:], "qe " + kk, False, True)
-            for b in range(4):
-                bank = BANK[4 * h + b]
-                o, i, w = x[:, b:512:4], T[bank][:, 0:128], "%s_%d" % (xk, b)
-                if b % 2:
-                    vs(o, i, 0.015625, None, A.mult, bank, w)
-                else:
-                    ac(o, i, bank, w, 0.015625)
-            a = slice(128 * h, 128 * h + 128)
-            qn, qns = T["qx%d" % (t + 1)], T["qxs%d" % (t + 1)]
-            key = "qx%d%s" % (t + 1, "LH"[h])
-            quant(qn[:, a], qns[:, a], x[:], " ".join("%s_%d" % (xk, b) for b in range(4)), key)
-            if t < R - 1:
-                score_mm(t + 1, h)
-                score_bits(h)
-                continue
-            mm(BANK[h], 128, T.qv[:], T.qvs[:], qn[:, a], qns[:, a], "qv " + key)
-            lst = [("y", T.oc[:, 512 * h:512 * h + 512], qn[:, a].bitcast(dt.uint8))]
-            lst += [("y", T.osc[4 * k:4 * k + 4, a], qns[32 * k:32 * k + 4, a]) for k in range(4)]
-            dmas("doc" + "lh"[h], lst, key, "")
-            ac(T.oaf[:, a], T.nw[:, 2048:2304].indirect(T.ga[:] if h else gl[:, 0:8]), "nwi " + ("ga" if h else "gl" + ts), "oa%d" % h)
-            ac(T.ys[:, a], T[BANK[h]][:, 0:128], BANK[h], "ys%d" % h)
-            dmas("dy" + "lh"[h], [("s", T.y[:, a], T.ys[:, a])], "ys%d" % h, "")
+            make_x(0)
+            make_z(1)
+            make_r(1)
+            make_x(1)
     dmas("doa", [("y", T.oa[:], T.oaf[0:128:16, :])], "oa0 oa1", "")
     for s in sorted(cnt):
         if known["g"].get(s, 0) < cnt[s]:

from concourse.mybir import dt, AluOpType, AxisListType, ActivationFunctionType

A = AluOpType
AF = ActivationFunctionType
R = 3
SCRATCH = {}
for _d, _l in (
        ("int32", "nx4:512 ep:512 e8:128 ep2:256 pp:128 ai0:128 ai:128 n4i:512 sl:256 slt:256 ip:8 iph:8 iy:2 k0:64 pc:32 ei:128 am:16"),
        ("float32", "p4:128 pr:256 pw:256 nw:2304 kf:64 cst:32 geo:32 ss:128 key:128 norm:16 c8:16 pg:256 pt:256 "
                    "ek:128 dd:128 yi:16 amc:16 tmp:128 jk:128 wk:112 bg:288 bt:288 val:16 oaf:256 ys:256"),
        ("bfloat16", "n4:512 nr:2048 i64:128 c64:128 et:2048 ut:512 vt:512 sb:256 nbf:256 at:256 f:1024 fa:1024 "
                     "co0:16 co1:16 ca0:16 ca1:16 xl0:512 xl1:512 xl2:512 xl3:512 xh0:512 xh1:512 xh2:512 xh3:512 "
                     "zl0:512 zl1:512 zl2:512 zh0:512 zh1:512 zh2:512"),
        ("uint16", "ul:8 lb:18 ou:16 nu:256 ga0:8 ga1:8 ga2:8 gl0:16 gl1:16 gl2:16")):
    for _s in _l.split():
        SCRATCH[_s.split(":")[0]] = ("sbuf", [128, int(_s.split(":")[1])], _d)
for _s in "qe:512 lw:512 qu:128 qy:128 qv:128 qx:256:4 qh:128:3 ql:128:3 qn:256:3".split():
    _p = _s.split(":")
    for _t in ([""] if len(_p) == 2 else ["%d" % k for k in range(int(_p[2]))]):
        SCRATCH[_p[0] + _t] = ("sbuf", [128, int(_p[1])], "float8_e4m3fn_x4")
        SCRATCH[_p[0] + "s" + _t] = ("sbuf", [128, int(_p[1])], "uint8")
BANK = ["b%d" % k for k in range(10, 18)]
for _s in BANK:
    SCRATCH[_s] = ("psum", [128, 512], "float32")
SEMAPHORES = ("cv cs ct cg dnx dal dx du dv dw dpr dnr dyl dyh doa docl doch dgl0 dgl1 dgl2".split()
              + [n + "%d" % t for n in ("rl", "ll", "rc", "lc", "rs", "ls", "rg", "lg") for t in range(R)])


def rank_program(g, core, T, topo):
    rank = T.rank_of(core)
    if rank is None:
        return
    nxt = T.cores[(rank + 1) % len(T.cores)]
    rid, pid, _ = topo.addr(nxt)
    mask, neng = topo.mask(core, nxt), len(topo.engines(core, nxt))
    V, S, P = g.vector, g.scalar, g.tensor
    eng = {"v": V, "s": S, "t": P, "g": g, "y": g.sync}
    csem = {"v": "cv", "s": "cs", "t": "ct", "g": "cg"}
    cnt, wr, rd = {}, {}, {}
    known = {q: {} for q in eng}

    def deps(q, r, w):
        toks = [wr[k] for k in r if k in wr]
        for k in w:
            toks += rd.get(k, []) + ([wr[k]] if k in wr else [])
        toks = [t for t in toks if known[q].get(t[0], 0) < t[1]]
        best = {}
        for t in toks:
            if t[0] not in best or best[t[0]][1] < t[1]:
                best[t[0]] = t
        for t in list(best.values()):
            if not any(o is not t and o[2].get(t[0], 0) >= t[1] for o in best.values()):
                eng[q].wait_ge(T.sem[t[0]], t[1])
        for t in toks:
            for s, n in list(t[2].items()) + [(t[0], t[1])]:
                known[q][s] = max(known[q].get(s, 0), n)

    def note(tok, r, w):
        for k in r:
            rd.setdefault(k, []).append(tok)
        for k in w:
            wr[k] = tok
            rd[k] = []

    def op(q, fn, r, w, more=""):
        r, w = r.split(), w.split()
        w = w + [k for k in r if k in BANK]
        deps(q, r, w)
        s = csem[q]
        cnt[s] = cnt.get(s, 0) + 1
        fn().then_inc(T.sem[s], 1)
        clk = dict(known[q])
        clk[s] = cnt[s]
        note((s, cnt[s], clk), r, w + more.split())

    def dmas(sem, lst, r, w):
        r, w = r.split(), w.split()
        qs = sorted(set(q for q, _, _ in lst))
        for q in qs:
            deps(q, r, w)
        for q, o, i in lst:
            cnt[sem] = cnt.get(sem, 0) + 16
            eng[q].dma_start(o, i).then_inc(T.sem[sem], 16)
        clk = {sem: cnt[sem]}
        for q in qs:
            for s, n in known[q].items():
                clk[s] = max(clk.get(s, 0), n)
        note((sem, cnt[sem], clk), r, w)

    def send(out, inp, k, t, r, lands):
        rs, ls, r = "r%s%d" % (k, t), "l%s%d" % (k, t), r.split()
        deps("g", r, [])
        g.remote_dma(out, inp, T.sem[rs], T.sem[ls], pid, rid, mask)
        for s in (ls, rs):
            cnt[s] = cnt.get(s, 0) + neng
        note((ls, cnt[ls], {}), r, [])
        note((rs, cnt[rs], {}), [], [lands])

    def vs(out, i, s1, s2, o1, r, w, o2=None):
        if o2 is None:
            op("v", lambda: V.tensor_scalar(out, i, s1, None, o1), r, w)
        else:
            op("v", lambda: V.tensor_scalar(out, i, s1, s2, o1, o2), r, w)

    def vt(out, a, b, o, r, w):
        op("v", lambda: V.tensor_tensor(out, a, b, o), r, w)

    def vc(out, i, r, w):
        op("v", lambda: V.tensor_copy(out, i), r, w)

    def ac(out, i, r, w, scale=None):
        if scale is None:
            op("s", lambda: S.activation(out, i, AF.Copy), r, w)
        else:
            op("s", lambda: S.activation(out, i, AF.Copy, scale=scale), r, w)

    def fill(ap, c, w):
        op("v", lambda: V.memset(ap, c), "", w)

    def quant(o, s, i, r, w):
        op("v", lambda: V.quantize_mx(o, s, i), r, w)

    def turn(o, i, r, w):
        op("v", lambda: V.transpose(o, i), r, w)

    def scan(o, d, first, r, w):
        op("v", lambda: V.tensor_tensor_scan(o, d, T.cst[:, 16:24], first, A.mult, A.add), r, w)

    def iota(o, pat, base, cm, w, small=False):
        if small:
            op("g", lambda: g.iota(o, pat, base, cm, allow_small_or_imprecise_dtypes=True), "", w)
        else:
            op("g", lambda: g.iota(o, pat, base, cm), "", w)

    def mm(bank, n, l, ls, rh, rs, r, start=True, stop=True):
        op("t", lambda: P.matmul_mx(T[bank][:, 0:n], l, ls, rh, rs, start, stop), r, bank if start else "", bank)

    k0, kf, wk = T.k0, T.kf, T.wk
    dmas("dnx", [("ys"[e // 2], T.nx4[0:32, 128 * e:128 * e + 128], T.nx[e:128:4, :]) for e in range(4)], "", "nx4")
    dmas("dx", [("y", T.xl0[:], T.x[:, 0:512]), ("s", T.xh0[:], T.x[:, 512:1024])], "", "xl0 xh0")
    dmas("du", [("y", T.ut[:], T.u[:])], "", "ut")
    fill(T.sl[:], 0, "sl")
    fill(T.c64[:], 64.0, "c64")
    dmas("dal", [("sy"[k % 2], T.sl[2 * k:128:16, 32 * k:32 * k + 32], T.al[16 * k:16 * k + 16, :]) for k in range(8)], "", "sl")
    dmas("dw", [("y", T.lw[:].bitcast(dt.uint8), T.wc[:]), ("s", T.lws[:], T.ws[:])], "", "lw")
    dmas("dv", [("y", T.vt[:], T.v[:])], "", "vt")

    iota(T.ip[:], [[0, 8]], 0, 1, "ip")
    iota(T.ai0[0:32, :], [[0, 2], [4, 64]], 0, 0, "ai0")
    iota(T.iph[:], [[1, 8]], 0, 1, "iph")
    iota(T.iy[:], [[2, 2]], 0, 16, "iy")
    op("g", lambda: g.affine_select(T.i64[:], T.c64[:], [[-1, 128]], A.is_equal, 0.0, 0, 1), "c64", "i64")
    iota(T.c8[:], [[0, 8], [64, 2]], -19, 0, "c8i", True)
    iota(T.et[:], [[0, 2048]], 0, 0, "et", True)
    for e in range(4):
        iota(T.key[:, 32 * e:32 * e + 16], [[0, 8], [512, 2]], -31 - 32 * e, 0, "key%d" % e, True)
        iota(T.key[:, 32 * e + 16:32 * e + 32], [[0, 8], [-512, 2]], 33 + 32 * e, 0, "key%d" % (e + 4), True)

    fill(T.cst[:, 0:8], 2.0 ** -5, "cst0")
    fill(T.cst[:, 8:16], 32.0, "cst1")
    fill(T.cst[:, 16:24], 0.0, "cst2")
    vs(k0[:, 0:1], T.ip[:, 0:1], 3, None, A.bitwise_and, "ip", "k0a")
    scan(T.geo[:, 0:8], T.cst[:, 0:8], 64.0, "cst0 cst2", "geo0")
    scan(T.geo[:, 8:16], T.cst[:, 8:16], 2.0 ** -9, "cst1 cst2", "geo1")
    vc(kf[:, 0:1], k0[:, 0:1], "k0a", "kfa")
    vs(k0[:, 8:16], T.ip[:], 14, None, A.bitwise_and, "ip", "k0b")
    for y in range(2):
        vc(T.ss[:, y:16:2], T.geo[:, 0:8], "geo0", "ss%d" % y)
    vs(k0[:, 24:32], T.iph[:], 1, None, A.bitwise_and, "iph", "k0c")
    vs(kf[:, 8:16], k0[:, 8:16], 8.0, None, A.mult, "k0b", "kfb")
    vs(T.ai[0:32, :], T.ai0[0:32, :], kf[0:32, 0:1], 65536.0, A.add, "ai0 kfa", "aix", A.mult)
    vc(T.ss[:, 16:32], T.ss[:, 0:16], "ss0 ss1", "ss2")
    vt(kf[:, 16:24], kf[:, 8:16], k0[:, 24:32], A.add, "kfb k0c", "kfc")
    vs(T.ai[0:32, :], T.ai[0:32, :], 7 * 4369.0, None, A.add, "aix", "ai")
    vc(T.ss[:, 32:64], T.ss[:, 0:32], "ss0 ss1 ss2", "ss3")
    vc(T.ul[:], kf[:, 16:24], "kfc", "ul")

    vs(T.e8[0:32, :], T.nx4[0:32, 384:512], 8.0, None, A.mult, "nx4", "e8")
    for e in range(4):
        a = slice(128 * e, 128 * e + 128)
        if e < 3:
            vs(T.ep[0:32, a], T.nx4[0:32, a], 9 - 4 * e, 7 << (4 * e), A.logical_shift_right, "nx4", "ep%d" % e, A.bitwise_and)
        else:
            vs(T.ep[0:32, a], T.e8[0:32, :], 7 << 12, None, A.bitwise_and, "e8", "ep3")
    vt(T.ep2[0:32, :], T.ep[0:32, 0:256], T.ep[0:32, 256:512], A.add, "ep0 ep1 ep2 ep3", "epx")
    vt(T.pp[0:32, :], T.ep2[0:32, 0:128], T.ep2[0:32, 128:256], A.add, "epx", "pp")
    vt(T.p4[0:32, :], T.pp[0:32, :], T.ai[0:32, :], A.add, "pp ai", "p4")
    lst = []
    for H in range(8):
        for b in range(2):
            z = (b + H) % 2
            lst.append(("sy"[b], T.pr[16 * H + z:16 * H + 16:2, :], T.p4[0:32, 64 * b:64 * b + 64]))
    dmas("dpr", lst, "p4", "pr")
    vs(T.n4i[0:32, :], T.nx4[0:32, :], 511, None, A.bitwise_and, "nx4", "n4i")
    vc(T.n4[0:32, :], T.n4i[0:32, :], "n4i", "n4")
    dmas("dnr", [("sy"[z], T.nr[16 * H + z:16 * H + 16:2, :], T.n4[0:32, :]) for H in range(8) for z in range(2)], "n4", "nr")
    for b in range(4):
        ac(T.et[:, 512 * b + b:512 * b + 512:4], T.i64[:], "i64 et", "et_%d" % b)

    def score_mm(t, h):
        a = slice(128 * h, 128 * h + 128)
        mm(BANK[h], 128, T.qy[:], T.qys[:], T["qx%d" % t][:, a], T["qxs%d" % t][:, a], "qy qys qx%d" % t + "LH"[h])

    def score_bits(h):
        vs(T.sb[:, 128 * h:128 * h + 128], T[BANK[h]][:, 0:128], 0.0, 0.5, A.is_gt, BANK[h], "sb%d" % h, A.subtract)

    def send_state(t):
        k = "qx%dL qx%dH" % (t, t)
        send(T["qn%d" % t][:].bitcast(dt.uint8), T["qx%d" % t][:].bitcast(dt.uint8), "c", t, k, "qnc%d" % t)
        send(T["qns%d" % t][:], T["qxs%d" % t][:], "s", t, k, "qns%d" % t)

    quant(T.qu[:], T.qus[:], T.ut[:], "ut", "qu")
    turn(T.slt[:], T.sl[:], "sl", "slt")
    vc(T.qy[:].bitcast(dt.uint32), T.qu[:].bitcast(dt.uint32).indirect(T.ul[:]), "qu ul", "qy")
    ac(T.qys[:], T.qus[:].indirect(T.ul[:]), "qu ul", "qys")
    quant(T.qx0[:, 0:128], T.qxs0[:, 0:128], T.xl0[:], "xl0", "qx0L")
    quant(T.qx0[:, 128:256], T.qxs0[:, 128:256], T.xh0[:], "xh0", "qx0H")
    iota(T.nw[:, 2048:2304], [[1, 256]], 0, 0, "nwi", True)
    send_state(0)
    score_mm(0, 0)
    score_mm(0, 1)
    vs(k0[:, 32:34], T.ip[:, 0:2], 4, None, A.logical_shift_right, "ip", "k0e")
    vc(T.lb[:, 0:16:2], T.slt[:, 0:256:34], "slt", "lb0")
    vc(T.lb[:, 1:16:2], T.slt[:, 16:256:34], "slt", "lb1")
    vs(k0[:, 16:17], k0[:, 32:33], 1, None, A.bitwise_and, "k0e", "k0d")
    vs(kf[:, 32:34], k0[:, 32:34], -254.0, None, A.mult, "k0e", "kfe")
    vs(T.c8[:], T.c8[:], 0.5, None, A.mult, "c8i", "c8")
    vc(kf[:, 40:41], k0[:, 16:17], "k0d", "kfd")
    vt(kf[:, 34:36], kf[:, 32:34], T.iy[:], A.add, "kfe iy", "kff")
    vc(T.ss[:, 64:128], T.ss[:, 0:64], "ss0 ss1 ss2 ss3", "ss4")
    vs(T.lb[:, 16:18], kf[:, 34:36], kf[:, 40:41], None, A.subtract, "kff kfd", "lbj")
    score_bits(0)
    score_bits(1)
    vc(T.norm[:, 0:16:2], T.geo[:, 8:16], "geo1", "norm0")
    vs(T.norm[:, 1:16:2], T.geo[:, 8:16], -1.0, None, A.mult, "geo1", "norm1")
    for r in range(4):
        (ac if r % 2 else vc)(T.pw[:, r:256:4], T.pr[:, 64 * r:64 * r + 64], "pr", "pw%d" % r)

    def prefetch_pick():
        ac(T.pg[:], T.pw[:].indirect(T.lb[:, 0:16]), "pw0 pw1 pw2 pw3 lb0 lb1", "pg")

    def prefetch_1():
        turn(T.pt[:], T.pg[:], "pg", "pt")
        vc(T.pc[:, 0:16], T.pt[:, 0:256:17], "pt", "pc0")
        vc(T.pc[:, 16:32:2], T.pt[:, 1:256:34], "pt", "pc1")
        vc(T.pc[:, 17:32:2], T.pt[:, 16:256:34], "pt", "pc2")

    def prefetch_2():
        vs(T.am[:], T.pc[:, 0:16], 16, None, A.logical_shift_right, "pc0", "am")
        for e in range(4):
            vs(T.ei[:, 32 * e:32 * e + 32], T.pc[:], 4 * e, 7, A.logical_shift_right, "pc0 pc1 pc2", "ei%d" % e, A.bitwise_and)
        vs(T.yi[:], T.am[:], 2.0 ** -8, 8.0, A.mult, "am", "yi", A.add)
        vt(T.ek[:], T.ei[:], T.key[:], A.add, "ei0 ei1 ei2 ei3 " + " ".join("key%d" % k for k in range(8)), "ek")
        vt(T.amc[:], T.yi[:], T.c8[:], A.add, "yi c8", "amc")
        vt(T.dd[:], T.ek[:], T.ss[:], A.mult, "ek ss0 ss1 ss2 ss3 ss4", "dd")

    def bits_pick():
        ac(T.bg[:, 160:288], T.sb[:].indirect(T.lb[:, 10:18]), "sb0 sb1 lb0 lb1 lbj", "bg1")
        vc(T.bg[:, 0:160], T.sb[:].indirect(T.lb[:, 0:10]), "sb0 sb1 lb0 lb1", "bg0")

    prefetch_pick()
    bits_pick()
    quant(T.qe[:], T.qes[:], T.et[:], "et et_0 et_1 et_2 et_3", "qe")
    for r in range(4):
        ac(T.nw[:, r:2048:4], T.nr[:, 512 * r:512 * r + 512], "nr", "nw%d" % r)
    NW = "nw0 nw1 nw2 nw3 nwi "
    prefetch_1()
    prefetch_2()

    bt, val, tmp = T.bt, T.val, T.tmp
    for t in range(R):
        ts = "%d" % t
        gl, ga = T["gl" + ts], T["ga" + ts]
        halves = (("f", T.f, [2, 3, 4, 5], "qx", "qx%dL qx%dH" % (t, t)), ("fa", T.fa, [6, 7, 0, 1], "qn", "qnc%d qns%d" % (t, t)))
        if t:
            bits_pick()
        for _, _, bk, q, k in halves:
            for b in range(4):
                a = slice(128 * b, 128 * b + 128)
                mm(BANK[bk[b]], 256, T.qe[:, a], T.qes[:, a], T[q + ts][:], T[q + "s" + ts][:], "qe " + k)
        turn(bt[:, 256:288], T.bg[:, 256:288], "bg1", "bte")
        vs(wk[:, 0:1], bt[:, 257:258], 64.0, 80.0, A.mult, "bte", "w0", A.add)
        op("s", lambda: S.activation(wk[:, 8:9], bt[:, 272:273], AF.Identity, bias=432.0, scale=-64.0), "bte", "w1")
        turn(bt[:, 0:256], T.bg[:, 0:256], "bg0 bg1", "bt")
        vs(val[:, 0:1], bt[:, 259:260], 32.0, wk[:, 0:1], A.mult, "bte w0", "val0", A.add)
        op("s", lambda: S.activation(val[:, 1:2], bt[:, 274:275], AF.Identity, bias=wk[:, 8:9], scale=-32.0), "bte w1", "val1")
        x0, x1, x2, o = wk[:, 32:46], wk[:, 48:62], wk[:, 64:78], T.ou

        def last(y):
            i = 14 + y
            vs(wk[:, 46 + y:47 + y], val[:, i:i + 1], (-1.0) ** y * 2.0 ** 31, wk[:, 16 + i:17 + i], A.mult, "val%d b3" % i, "l%d" % y, A.add)

        def last2(y):
            i = 14 + y
            vs(o[:, i:i + 1], wk[:, 46 + y:47 + y], T.yi[:, i:i + 1], 256.0, A.min, "l%d yi" % y, "ou%d" % y, A.mult)

        for i in range(14):
            c, d = slice(8 * i, 8 * i + 8), T.dd[:, i:128:16]
            me, sg, new = val[:, i:i + 1], bt[:, 17 * i:17 * i + 1], val[:, i + 2:i + 3]
            if i % 2:
                op("s", lambda: S.activation(tmp[:, c], d, AF.Abs, bias=me, scale=sg), "dd bt val%d" % i, "tmp%d" % i)
                op("s", lambda: S.activation(T.jk[:, c], tmp[:, c], AF.Relu, bias=16.0 * 32.0 ** -(i // 2), scale=-1.0, accum_out=new),
                   "tmp%d" % i, "jk%d val%d" % (i, i + 2))
            else:
                vs(tmp[:, c], d, sg, me, A.mult, "dd bt val%d" % i, "tmp%d" % i, A.subtract)
                if i == 2:
                    vt(wk[:, 16:32], bt[:, 0:256:17], T.amc[:], A.add, "bt amc", "b3")
                op("v", lambda: V.tensor_reduce(new, tmp[:, c], AxisListType.X, A.min, apply_absolute_value=True), "tmp%d" % i, "val%d" % (i + 2))
        vt(x0, val[:, 0:14], T.norm[:, 0:14], A.mult, "norm0 norm1 " + " ".join("val%d" % i for i in range(14)), "t1")
        last(0)
        vt(x1, x0, wk[:, 16:30], A.add, "t1 b3", "t2")
        last2(0)
        vt(x2, x1, T.yi[:, 0:14], A.min, "t2 yi", "t3")
        last(1)
        vs(o[:, 0:14], x2, 256.0, None, A.mult, "t3", "ou")
        last2(1)
        vc(T.nu[:], T.nw[:].indirect(o[:]), NW + "ou ou0 ou1", "nu")
        if t < R - 1:
            ac(T.nbf[:], T.nw[:].indirect(o[:]), NW + "ou ou0 ou1", "nbf")
        dmas("dgl" + ts, [("ys"[k % 2], gl[16 * k:16 * k + 16, :], T.nu[2 * k:128:16, 32 * k:32 * k + 32]) for k in range(8)], "nu", "gl" + ts)
        if t < R - 1:
            co = T["co" + ts]
            turn(T.at[:], T.nbf[:], "nbf", "at")
            vc(co[:], T.at[:, 0:256:17], "at", "co" + ts)
            send(T["ca" + ts][:], co[:], "l", t, "co" + ts, "ca" + ts)
        send(ga[:], gl[:, 8:16], "g", t, "gl" + ts, "ga" + ts)
        for n, f, bk, _, _ in halves:
            for b in range(4):
                bank = BANK[bk[b]]
                fo, fi = f[:, 256 * b:256 * b + 256], T[bank][:, 0:256]
                if b % 2:
                    vs(fo, fi, 0.015625, None, A.mult, bank, "%s_%d" % (n, b))
                else:
                    ac(fo, fi, bank, "%s_%d" % (n, b), 0.015625)
            if n == "f" and t < R - 1:
                if t == 0:
                    vs(k0[:, 40:41], T.ip[:, 0:1], 8, None, A.bitwise_and, "ip", "k0m")
                    vs(kf[:, 56:57], k0[:, 40:41], 0.0, None, A.is_equal, "k0m", "mlo")
                    vs(kf[:, 57:58], k0[:, 40:41], 0.0, None, A.is_gt, "k0m", "mhi")
                vs(wk[:, 80:96], co[:], kf[:, 56:57], None, A.mult, "mlo co" + ts, "m1")

        def make_z(h):
            k, n, off, ok = "lh"[h] + ts, ("f", "fa")[h], (gl[:, 0:8], ga[:])[h], ("gl", "ga")[h] + ts
            z = T["z" + k]
            for b in range(4):
                (vc if b < 2 else ac)(z[:, b:512:4], T[n][:, 256 * b:256 * b + 256].indirect(off), "%s_%d %s" % (n, b, ok), "z%s_%d" % (k, b))
            quant(T["q" + k][:], T["q" + "lh"[h] + "s" + ts][:], z[:], " ".join("z%s_%d" % (k, b) for b in range(4)), "q" + k)

        def make_r(h):
            q, qs, kk = T["q" + "lh"[h] + ts], T["q" + "lh"[h] + "s" + ts], "q" + "lh"[h] + ts
            for b in range(4):
                a = slice(128 * b, 128 * b + 128)
                mm(BANK[4 * h + b], 128, T.lw[:, a], T.lws[:, a], q[:], qs[:], "lw " + kk, True, False)
                mm(BANK[4 * h + b], 128, T.qe[:, a], T.qes[:, a], q[:], qs[:], "qe " + kk, False, True)

        def make_x(h):
            a, xk = slice(128 * h, 128 * h + 128), "x%s%d" % ("lh"[h], t + 1)
            for b in range(4):
                bank = BANK[4 * h + b]
                xo, xi, w = T[xk][:, b:512:4], T[bank][:, 0:128], "%s_%d" % (xk, b)
                if b % 2:
                    vs(xo, xi, 0.015625, None, A.mult, bank, w)
                else:
                    ac(xo, xi, bank, w, 0.015625)
            qn, qns, key = T["qx%d" % (t + 1)], T["qxs%d" % (t + 1)], "qx%d%s" % (t + 1, "LH"[h])
            quant(qn[:, a], qns[:, a], T[xk][:], " ".join("%s_%d" % (xk, b) for b in range(4)), key)
            if t < R - 1:
                score_mm(t + 1, h)
                return
            mm(BANK[h], 128, T.qv[:], T.qvs[:], qn[:, a], qns[:, a], "qv " + key)
            lst = [("y", T.oc[:, 512 * h:512 * h + 512], qn[:, a].bitcast(dt.uint8))]
            lst += [("y", T.osc[4 * k:4 * k + 4, a], qns[32 * k:32 * k + 4, a]) for k in range(4)]
            dmas("doc" + "lh"[h], lst, key, "")
            ac(T.oaf[:, a], T.nw[:, 2048:2304].indirect(ga[:] if h else gl[:, 0:8]), "nwi " + ("ga" if h else "gl") + ts, "oa%d" % h)
            ac(T.ys[:, a], T[BANK[h]][:, 0:128], BANK[h], "ys%d" % h)
            dmas("dy" + "lh"[h], [("s", T.y[:, a], T.ys[:, a])], "ys%d" % h, "")

        make_z(0)
        make_r(0)
        if t < R - 1:
            vs(wk[:, 96:112], T["ca" + ts][:], kf[:, 57:58], None, A.mult, "mhi ca" + ts, "m2")
            vt(wk[:, 32:48], wk[:, 80:96], wk[:, 96:112], A.add, "m1 m2", "t1 l0 l1")
            vc(T.lb[:, 0:16], wk[:, 32:48], "t1", "lb0 lb1")
            prefetch_pick()
            make_x(0)
            prefetch_1()
            make_z(1)
            make_r(1)
            score_bits(0)
            prefetch_2()
            make_x(1)
            send_state(t + 1)
            score_bits(1)
        else:
            quant(T.qv[:], T.qvs[:], T.vt[:], "vt", "qv")
            make_x(0)
            make_z(1)
            make_r(1)
            make_x(1)
    dmas("doa", [("y", T.oa[:], T.oaf[0:128:16, :])], "oa0 oa1", "")
    for s in sorted(cnt):
        if known["g"].get(s, 0) < cnt[s]:
            g.wait_ge(T.sem[s], cnt[s])
